import numpy as np
import ml_dtypes


def mxq(x, axis, fmt="e4m3"):
    dtype, down = {"e4m3": (ml_dtypes.float8_e4m3fn, 7), "e5m2": (ml_dtypes.float8_e5m2, 14)}[fmt]
    v = np.moveaxis(np.asarray(x, np.float32).astype(ml_dtypes.bfloat16).astype(np.float64), axis, -1)
    blocks = v.reshape(v.shape[:-1] + (-1, 32))
    amax = np.abs(blocks).max(-1, keepdims=True)
    byte = np.maximum(np.where(amax > 0, np.frexp(amax)[1] - 1 + 127, 0) - down, 1)
    scale = np.exp2(byte - 127.0)
    codes = (blocks / scale).astype(np.float32).astype(dtype).astype(np.float64)
    return np.moveaxis((codes * scale).reshape(v.shape), -1, axis)


WIDE = False


def mx_kscale(k):
    if not WIDE:
        return np.ones(k)
    levels = np.array([10, -10, 5, -5, 0])
    if k % 512:
        return np.exp2(np.random.permutation(np.resize(levels, k // 32))).repeat(32)
    a = np.empty((k // 512, 16))
    for p in range(k // 512):
        a[p, :8] = np.random.permutation(np.resize(levels, 8))
        for g in range(8):
            far = levels[np.abs(levels - a[p, g]) >= 10]
            a[p, g + 8] = far[np.random.randint(len(far))]
    return np.exp2(a.ravel()).repeat(32)


def f64(x):
    return np.asarray(x).astype(np.float64)


def striped(idx):
    return np.tile(idx.reshape(-1, 16).T, (8, 1)).astype(np.uint16)


def unstriped(offs):
    return offs[:16].T.reshape(-1).astype(np.int64)


E2M1 = np.array([0.0, 0.5, 1.0, 1.5, 2.0, 3.0, 4.0, 6.0, -0.0, -0.5, -1.0, -1.5, -2.0, -3.0, -4.0, -6.0])


def pack_weight(w, fmt):
    k, n = w.shape
    w = f64(np.asarray(w, np.float32).astype(ml_dtypes.bfloat16)).reshape(k // 32, 32, n)
    amax = np.abs(w).max(1)
    if fmt == "e4m3":
        byte = np.frexp(amax)[1] - 1 + 127 - 7
    else:
        mant, ex = np.frexp(amax / 6.0)
        byte = np.where(mant > 0.5, ex, ex - 1) + 127
    byte = np.clip(np.where(amax > 0, byte, 1), 1, 254)
    scaled = (w * np.exp2(127.0 - byte)[:, None, :]).reshape(k, n).astype(np.float32)
    by_word = np.ascontiguousarray(scaled.reshape(k // 512, 128, 4, n).transpose(0, 1, 3, 2))
    if fmt == "e4m3":
        words = by_word.astype(ml_dtypes.float8_e4m3fn).view(np.uint8)
    else:
        c = by_word.astype(ml_dtypes.float4_e2m1fn).view(np.uint8) & 0xF
        words = (c[..., 0::2] | (c[..., 1::2] << 4)).reshape(k // 512, 128, 2 * n)
    return np.ascontiguousarray(words), np.ascontiguousarray(byte.astype(np.uint8).reshape(k // 512, 16, n))


def unpack_weight(words, scales, fmt):
    g, _, n = scales.shape
    words = np.ascontiguousarray(words).reshape(g, 128, n, -1)
    if fmt == "e4m3":
        vals = words.view(ml_dtypes.float8_e4m3fn).astype(np.float64)
    else:
        nib = np.empty((g, 128, n, 4), np.uint8)
        nib[..., 0::2] = words & 0xF
        nib[..., 1::2] = words >> 4
        vals = E2M1[nib]
    vals = vals * np.repeat(np.exp2(scales.astype(np.float64) - 127.0), 8, axis=1)[..., None]
    return vals.transpose(0, 1, 3, 2).reshape(g * 512, n)


def gelu(v):
    return 0.5 * v * (1.0 + np.tanh(np.sqrt(2.0 / np.pi) * (v + 0.044715 * v**3)))


K, H, N, T, S = 1536, 512, 384, 2048, 1024

def setup_inputs():
    n = np.random.standard_normal
    s = mx_kscale(K)[:, None]
    u = mx_kscale(H)[:, None]
    tab_words, tab_scales = pack_weight(n((K, T)) * s, "e4m3")
    offs = striped(np.random.permutation(T)[:S])
    wa = (n((K, H)) / np.sqrt(K) / s * u.T).astype(np.float32)
    ba = (0.5 * n(H) * u[:, 0]).astype(np.float32)
    wb_words, wb_scales = pack_weight(n((K, H)) / np.sqrt(K) / s, "e2m1")
    gT = (1.0 / (1.0 + np.exp(-n((H, T))))).astype(np.float32)
    wo = (1.5 * n((H, N)) / np.sqrt(H) / u).astype(np.float32)
    bo = (0.5 * n(N)).astype(np.float32)
    return {"tab_words": tab_words, "tab_scales": tab_scales, "offs": offs,
            "wa": wa, "ba": ba, "wb_words": wb_words, "wb_scales": wb_scales,
            "gT": gT, "wo": wo, "bo": bo}

def reference(tab_words, tab_scales, offs, wa, ba, wb_words, wb_scales, gT, wo, bo):
    v = unpack_weight(tab_words, tab_scales, "e4m3")[:, unstriped(offs)]
    g = f64(gT)[:, unstriped(offs)]
    a = mxq(f64(wa), 0, "e4m3").T @ v
    b = unpack_weight(wb_words, wb_scales, "e2m1").T @ v
    h = (a + f64(ba)[:, None]) * b * g
    y = mxq(f64(wo), 0, "e4m3").T @ mxq(h, 0, "e4m3")
    return y + f64(bo)[:, None]

@@ -1,0 +1,293 @@
+from contextlib import ExitStack
+
+import concourse.mybir as mybir
+
+K, H, N, T, S = 1536, 512, 384, 2048, 1024
+FLOPS = 2 * S * (2 * K * H + H * N)
+
+F32 = mybir.dt.float32
+BF16 = mybir.dt.bfloat16
+I32 = mybir.dt.int32
+U32 = mybir.dt.uint32
+U16 = mybir.dt.uint16
+U8 = mybir.dt.uint8
+FP8X4 = mybir.dt.float8_e4m3fn_x4
+FP4X4 = mybir.dt.float4_e2m1fn_x4
+MULT = mybir.AluOpType.mult
+IDENT = mybir.ActivationFunctionType.Identity
+
+P = 128
+PASSES = K // 512
+SLOTS = 4
+HALF = 512
+BANK_TOKENS = 128
+OUT_TILES = N // P
+OUT_CHUNKS = [128, 256, 256, 256, 128]
+
+
+def tile_list_contact_gated_update_kernel(
+    tc, tab_words, tab_scales, offs, wa, ba, wb_words, wb_scales, gT, wo, bo, out
+):
+    nc = tc.nc
+    with ExitStack() as ctx:
+        keep = ctx.enter_context(tc.tile_pool(name="keep", bufs=1))
+        ring = ctx.enter_context(tc.tile_pool(name="ring", bufs=2))
+        psum = ctx.enter_context(tc.psum_pool(name="psum", bufs=8))
+
+        def sb(name, shape, dtype):
+            return keep.tile(shape, dtype, name=name, align_bytes=64)
+
+        offsets = keep.tile([P, S // 16], U16, name="offsets")
+        nc.sync.dma_start(offsets[:], offs)
+
+        def picks(first, count):
+            return offsets[:, first // 16 : (first + count) // 16]
+
+        scale_win = sb("scale_win", [P, T // 4], I32)
+        nc.gpsimd.memset(scale_win[:], 0)
+
+        def load_tab_scales():
+            for quad in range(4):
+                nc.sync.dma_start(
+                    scale_win[32 * quad : 32 * quad + 4 * PASSES, :],
+                    tab_scales[:, 4 * quad : 4 * quad + 4, :].bitcast(I32),
+                )
+
+        wbs_raw = sb("wbs_raw", [P, PASSES, H // 4], I32)
+        nc.vector.memset(wbs_raw[:], 0)
+
+        def load_wb_scales():
+            for quad in range(4):
+                nc.sync.dma_start(
+                    wbs_raw[32 * quad : 32 * quad + 4, :, :],
+                    wb_scales[:, 4 * quad : 4 * quad + 4, :].bitcast(I32).rearrange("a r c -> r a c"),
+                )
+
+        ba_cols = [sb(f"ba{t}", [P, 1], F32) for t in range(SLOTS)]
+        ba_view = ba.rearrange("(q t u o) -> t q u o", t=SLOTS, u=8, o=1)
+        bo_cols = sb("bo_cols", [P, OUT_TILES], F32)
+
+        def load_ba(t):
+            with nc.allow_non_contiguous_dma(reason="one bias value to a partition"):
+                nc.sync.dma_start(ba_cols[t][:], ba_view[t])
+
+        def load_bo():
+            with nc.allow_non_contiguous_dma(reason="one bias value to a partition"):
+                nc.sync.dma_start(bo_cols[:], bo.rearrange("(c p) -> p c", p=P))
+
+        wa_raw = [sb(f"wa_raw{a}", [P, SLOTS, H], F32) for a in range(PASSES)]
+        tab = [sb(f"tab{a}", [P, T], I32) for a in range(PASSES)]
+        wbw_raw = sb("wbw_raw", [P, PASSES, H // 2], I32)
+        gates = [sb(f"gates{t}", [P, T], F32) for t in range(SLOTS)]
+        wo_raw = sb("wo_raw", [P, SLOTS, N], F32)
+
+        def load_wa(a):
+            nc.sync.dma_start(
+                wa_raw[a][:], wa[512 * a : 512 * (a + 1), :].rearrange("(p j) c -> p j c", j=4)
+            )
+
+        def load_tab(a):
+            nc.sync.dma_start(tab[a][:], tab_words[a].rearrange("p t i -> p (t i)").bitcast(I32))
+
+        load_wa(0)
+        load_wa(1)
+        load_tab_scales()
+        load_tab(0)
+        nc.sync.dma_start(wbw_raw[:], wb_words.bitcast(I32).rearrange("a p c -> p a c"))
+        load_wa(2)
+        load_wb_scales()
+        load_tab(1)
+        load_ba(0)
+        load_ba(1)
+        load_tab(2)
+        load_ba(2)
+        load_ba(3)
+
+        v_scales = sb("v_scales", [P, S // 4], I32)
+        nc.vector.tensor_copy(
+            v_scales[:].bitcast(U8), scale_win[:].bitcast(U8).indirect(offsets[:])
+        )
+        v_scales_low = sb("v_scales_low", [P, PASSES - 1, S // 4], I32)
+        nc.vector.memset(v_scales_low[:], 0)
+
+        g_view = gT.rearrange("(q t u) c -> t q u c", t=SLOTS, u=8)
+        wo_view = wo.rearrange("(q t u) n -> t q u n", t=SLOTS, u=8)
+        nc.sync.dma_start(gates[0][:], g_view[0])
+        for a in range(1, PASSES):
+            nc.gpsimd.dma_start(v_scales_low[0:112, a - 1, :], v_scales[4 * a : 4 * a + 112, :])
+        for t in range(1, SLOTS):
+            nc.sync.dma_start(gates[t][:], g_view[t])
+        load_bo()
+        for t in range(SLOTS):
+            nc.sync.dma_start(wo_raw[:, t, :], wo_view[t])
+
+        wa_bf = [sb(f"wa_bf{a}", [P, SLOTS, P * 4], BF16) for a in range(PASSES)]
+        wa_codes = [sb(f"wa_codes{a}", [P, H], U32) for a in range(PASSES)]
+        wa_scales = [sb(f"wa_scales{a}", [P, H], U8) for a in range(PASSES)]
+        v_words = [sb(f"v_words{a}", [P, S], U32) for a in range(PASSES)]
+
+        def round_wa(a):
+            src = wa_raw[a][:].rearrange("p j (q t u) -> p t q u j", t=SLOTS, u=8)
+            for t in range(SLOTS):
+                nc.scalar.copy(
+                    wa_bf[a][:, t, :].rearrange("p (q u j) -> p q u j", u=8, j=4), src[:, t]
+                )
+
+        def quantise_wa(a):
+            nc.vector.quantize_mx(
+                out=wa_codes[a][:].bitcast(FP8X4),
+                scales=wa_scales[a][:],
+                in_=wa_bf[a][:].rearrange("p t c -> p (t c)"),
+            )
+
+        def gather_words(a, half):
+            nc.vector.tensor_copy(
+                v_words[a][:, half * HALF : (half + 1) * HALF],
+                tab[a][:].bitcast(U32).indirect(picks(half * HALF, HALF)),
+            )
+
+        a_banks = {}
+        for t in range(SLOTS):
+            for half in range(2):
+                a_banks[t, half] = psum.tile([P, HALF], F32, name="bank")
+
+        def a_pass(a, t, half):
+            cols = slice(half * HALF, (half + 1) * HALF)
+            nc.tensor.matmul_mx(
+                out=a_banks[t, half][:],
+                lhsT=wa_codes[a][:, t * P : (t + 1) * P].bitcast(FP8X4),
+                lhsT_scale=wa_scales[a][:, t * P : (t + 1) * P],
+                rhs=v_words[a][:, cols].bitcast(FP8X4),
+                rhs_scale=v_scales[4 * a : P, :].bitcast(U8)[:, cols],
+                start=(a == 0),
+                stop=(a == PASSES - 1),
+            )
+
+        wb_codes = sb("wb_codes", [P, PASSES, H // 2], I32)
+        wb_planes = sb("wb_planes", [P, PASSES, H // 4], I32)
+
+        round_wa(0)
+        round_wa(1)
+        round_wa(2)
+        quantise_wa(0)
+        gather_words(0, 0)
+        gather_words(0, 1)
+        for half in range(2):
+            for t in range(SLOTS):
+                a_pass(0, t, half)
+        quantise_wa(1)
+        nc.vector.tensor_copy(
+            wb_codes[:].rearrange("p a (t q w) -> p a t q w", t=SLOTS, w=4),
+            wbw_raw[:].rearrange("p a (q t w) -> p a t q w", t=SLOTS, w=4),
+        )
+        nc.vector.tensor_copy(
+            wb_planes[:].rearrange("p a (t q w) -> p a t q w", t=SLOTS, w=2),
+            wbs_raw[:].rearrange("p a (q t w) -> p a t q w", t=SLOTS, w=2),
+        )
+        gather_words(1, 0)
+        gather_words(1, 1)
+        for half in range(2):
+            for t in range(SLOTS):
+                a_pass(1, t, half)
+        quantise_wa(2)
+        gather_words(2, 0)
+        gather_words(2, 1)
+
+        a_biased = sb("a_biased", [P, SLOTS, S], F32)
+        gated = sb("gated", [P, SLOTS, S], F32)
+
+        def gate(t, first, count):
+            cols = slice(first, first + count)
+            nc.vector.tensor_tensor(
+                gated[:, t, cols], gates[t][:].indirect(picks(first, count)), a_biased[:, t, cols], MULT
+            )
+
+        for t in range(SLOTS):
+            for half in range(2):
+                a_pass(PASSES - 1, t, half)
+                nc.scalar.activation(
+                    a_biased[:, t, half * HALF : (half + 1) * HALF],
+                    a_banks[t, half][:],
+                    IDENT,
+                    bias=ba_cols[t][:],
+                )
+            if t < SLOTS - 1:
+                gate(t, 0, HALF)
+                gate(t, HALF, HALF)
+
+        b_banks = []
+        for c in range(S // BANK_TOKENS):
+            cols = slice(c * BANK_TOKENS, (c + 1) * BANK_TOKENS)
+            bank = psum.tile([P, SLOTS, BANK_TOKENS], F32, name="bank")
+            b_banks.append(bank)
+            for t in range(SLOTS):
+                for a in range(PASSES):
+                    plane = v_scales[:] if a == 0 else v_scales_low[:, a - 1, :]
+                    nc.tensor.matmul_mx(
+                        out=bank[:, t, :],
+                        lhsT=wb_codes[:, a, 64 * t : 64 * (t + 1)].bitcast(U8).bitcast(FP4X4),
+                        lhsT_scale=wb_planes[:, a, 32 * t : 32 * (t + 1)].bitcast(U8),
+                        rhs=v_words[a][:, cols].bitcast(FP8X4),
+                        rhs_scale=plane.bitcast(U8)[:, cols],
+                        start=(a == 0),
+                        stop=(a == PASSES - 1),
+                    )
+
+        result = sb("result", [P, OUT_TILES, S], F32)
+        out_view = out.rearrange("(c p) j -> p c j", p=P)
+        starts = [sum(OUT_CHUNKS[:i]) for i in range(len(OUT_CHUNKS))]
+        h_bf, codes, scales = {}, {}, {}
+
+        def make_h(i):
+            lead = N if i == 0 else 0
+            width = lead + OUT_CHUNKS[i]
+            h_bf[i] = ring.tile([P, width, SLOTS], BF16, name="h_bf", align_bytes=64)
+            codes[i] = sb(f"codes{i}", [P, width], U32)
+            scales[i] = sb(f"scales{i}", [P, width], U8)
+            if i == 0:
+                nc.scalar.copy(h_bf[0][:, 0:N, :], wo_raw[:].rearrange("p t n -> p n t"))
+            for j in range(OUT_CHUNKS[i] // BANK_TOKENS):
+                first = starts[i] + j * BANK_TOKENS
+                local = lead + j * BANK_TOKENS
+                nc.vector.tensor_tensor(
+                    h_bf[i][:, local : local + BANK_TOKENS, :].rearrange("p (n i) t -> p n t i", i=2),
+                    b_banks[first // BANK_TOKENS][:].rearrange("p t (n i) -> p n t i", i=2),
+                    gated[:, :, first : first + BANK_TOKENS].rearrange("p t (n i) -> p n t i", i=2),
+                    MULT,
+                )
+
+        def finish(i):
+            lead = N if i == 0 else 0
+            count = OUT_CHUNKS[i]
+            cols = slice(starts[i], starts[i] + count)
+            nc.vector.quantize_mx(
+                out=codes[i][:].bitcast(FP8X4),
+                scales=scales[i][:],
+                in_=h_bf[i][:].rearrange("p n t -> p (n t)"),
+            )
+            per_bank = 512 // count
+            bank = None
+            for c in range(OUT_TILES):
+                if c % per_bank == 0:
+                    bank = psum.tile([P, per_bank, count], F32, name="bank")
+                nc.tensor.matmul_mx(
+                    out=bank[:, c % per_bank, :],
+                    lhsT=codes[0][:, c * P : (c + 1) * P].bitcast(FP8X4),
+                    lhsT_scale=scales[0][:, c * P : (c + 1) * P],
+                    rhs=codes[i][:, lead : lead + count].bitcast(FP8X4),
+                    rhs_scale=scales[i][:, lead : lead + count],
+                    start=True,
+                    stop=True,
+                )
+                nc.scalar.activation(
+                    result[:, c, cols], bank[:, c % per_bank, :], IDENT, bias=bo_cols[:, c : c + 1]
+                )
+            nc.sync.dma_start(out_view[:, :, cols], result[:, :, cols])
+
+        for first in range(0, S, 256):
+            gate(SLOTS - 1, first, 256)
+        for i in range(len(OUT_CHUNKS)):
+            make_h(i)
+            if i > 0:
+                finish(i - 1)
+        finish(len(OUT_CHUNKS) - 1)

@@ -1,6 +1,7 @@
 from contextlib import ExitStack
 
 import concourse.mybir as mybir
+from concourse.masks import make_identity
 
 K, H, N, T, S = 1536, 512, 384, 2048, 1024
 FLOPS = 2 * S * (2 * K * H + H * N)
@@ -20,7 +21,6 @@ P = 128
 PASSES = K // 512
 SLOTS = 4
 HALF = 512
-BANK_TOKENS = 128
 OUT_TILES = N // P
 OUT_CHUNKS = [128, 256, 256, 256, 128]
 
@@ -44,42 +44,24 @@ def tile_list_contact_gated_update_kernel(
             return offsets[:, first // 16 : (first + count) // 16]
 
         scale_win = sb("scale_win", [P, T // 4], I32)
-        nc.gpsimd.memset(scale_win[:], 0)
-
-        def load_tab_scales():
-            for quad in range(4):
-                nc.sync.dma_start(
-                    scale_win[32 * quad : 32 * quad + 4 * PASSES, :],
-                    tab_scales[:, 4 * quad : 4 * quad + 4, :].bitcast(I32),
-                )
-
         wbs_raw = sb("wbs_raw", [P, PASSES, H // 4], I32)
+        bias_rows = sb("bias_rows", [P, P], F32)
+        identity = sb("identity", [P, P], F32)
+        v_scales = sb("v_scales", [P, S // 4], I32)
+        v_scales_low = sb("v_scales_low", [P, PASSES - 1, S // 4], I32)
+        nc.gpsimd.memset(scale_win[:], 0)
+        nc.vector.memset(bias_rows[:], 0.0)
         nc.vector.memset(wbs_raw[:], 0)
-
-        def load_wb_scales():
-            for quad in range(4):
-                nc.sync.dma_start(
-                    wbs_raw[32 * quad : 32 * quad + 4, :, :],
-                    wb_scales[:, 4 * quad : 4 * quad + 4, :].bitcast(I32).rearrange("a r c -> r a c"),
-                )
-
-        ba_cols = [sb(f"ba{t}", [P, 1], F32) for t in range(SLOTS)]
-        ba_view = ba.rearrange("(q t u o) -> t q u o", t=SLOTS, u=8, o=1)
-        bo_cols = sb("bo_cols", [P, OUT_TILES], F32)
-
-        def load_ba(t):
-            with nc.allow_non_contiguous_dma(reason="one bias value to a partition"):
-                nc.sync.dma_start(ba_cols[t][:], ba_view[t])
-
-        def load_bo():
-            with nc.allow_non_contiguous_dma(reason="one bias value to a partition"):
-                nc.sync.dma_start(bo_cols[:], bo.rearrange("(c p) -> p c", p=P))
+        nc.vector.memset(v_scales_low[:], 0)
+        make_identity(nc, identity[:])
 
         wa_raw = [sb(f"wa_raw{a}", [P, SLOTS, H], F32) for a in range(PASSES)]
         tab = [sb(f"tab{a}", [P, T], I32) for a in range(PASSES)]
         wbw_raw = sb("wbw_raw", [P, PASSES, H // 2], I32)
         gates = [sb(f"gates{t}", [P, T], F32) for t in range(SLOTS)]
         wo_raw = sb("wo_raw", [P, SLOTS, N], F32)
+        g_view = gT.rearrange("(q t u) c -> t q u c", t=SLOTS, u=8)
+        wo_view = wo.rearrange("(q t u) n -> t q u n", t=SLOTS, u=8)
 
         def load_wa(a):
             nc.sync.dma_start(
@@ -91,33 +73,38 @@ def tile_list_contact_gated_update_kernel(
 
         load_wa(0)
         load_wa(1)
-        load_tab_scales()
+        for quad in range(4):
+            nc.sync.dma_start(
+                scale_win[32 * quad : 32 * quad + 4 * PASSES, :],
+                tab_scales[:, 4 * quad : 4 * quad + 4, :].bitcast(I32),
+            )
+        nc.sync.dma_start(
+            bias_rows[0:SLOTS, :].rearrange("t (q u) -> t q u", u=8),
+            ba.rearrange("(q t u) -> t q u", t=SLOTS, u=8),
+        )
+        nc.sync.dma_start(
+            bias_rows[SLOTS : SLOTS + OUT_TILES, :], bo.rearrange("(c p) -> c p", p=P)
+        )
         load_tab(0)
-        nc.sync.dma_start(wbw_raw[:], wb_words.bitcast(I32).rearrange("a p c -> p a c"))
         load_wa(2)
-        load_wb_scales()
         load_tab(1)
-        load_ba(0)
-        load_ba(1)
         load_tab(2)
-        load_ba(2)
-        load_ba(3)
 
-        v_scales = sb("v_scales", [P, S // 4], I32)
         nc.vector.tensor_copy(
             v_scales[:].bitcast(U8), scale_win[:].bitcast(U8).indirect(offsets[:])
         )
-        v_scales_low = sb("v_scales_low", [P, PASSES - 1, S // 4], I32)
-        nc.vector.memset(v_scales_low[:], 0)
 
-        g_view = gT.rearrange("(q t u) c -> t q u c", t=SLOTS, u=8)
-        wo_view = wo.rearrange("(q t u) n -> t q u n", t=SLOTS, u=8)
         nc.sync.dma_start(gates[0][:], g_view[0])
+        for quad in range(4):
+            nc.sync.dma_start(
+                wbs_raw[32 * quad : 32 * quad + 4, :, :],
+                wb_scales[:, 4 * quad : 4 * quad + 4, :].bitcast(I32).rearrange("a r c -> r a c"),
+            )
+        nc.sync.dma_start(wbw_raw[:], wb_words.bitcast(I32).rearrange("a p c -> p a c"))
         for a in range(1, PASSES):
-            nc.gpsimd.dma_start(v_scales_low[0:112, a - 1, :], v_scales[4 * a : 4 * a + 112, :])
+            nc.sync.dma_start(v_scales_low[0:112, a - 1, :], v_scales[4 * a : 4 * a + 112, :])
         for t in range(1, SLOTS):
             nc.sync.dma_start(gates[t][:], g_view[t])
-        load_bo()
         for t in range(SLOTS):
             nc.sync.dma_start(wo_raw[:, t, :], wo_view[t])
 
@@ -146,6 +133,8 @@ def tile_list_contact_gated_update_kernel(
                 tab[a][:].bitcast(U32).indirect(picks(half * HALF, HALF)),
             )
 
+        bias_bank = psum.tile([P, P], F32, name="bank")
+        biases = sb("biases", [P, 8], F32)
         a_banks = {}
         for t in range(SLOTS):
             for half in range(2):
@@ -166,8 +155,20 @@ def tile_list_contact_gated_update_kernel(
         wb_codes = sb("wb_codes", [P, PASSES, H // 2], I32)
         wb_planes = sb("wb_planes", [P, PASSES, H // 4], I32)
 
+        def reorder_wb():
+            nc.vector.tensor_copy(
+                wb_codes[:].rearrange("p a (t q w) -> p a t q w", t=SLOTS, w=4),
+                wbw_raw[:].rearrange("p a (q t w) -> p a t q w", t=SLOTS, w=4),
+            )
+            nc.vector.tensor_copy(
+                wb_planes[:].rearrange("p a (t q w) -> p a t q w", t=SLOTS, w=2),
+                wbs_raw[:].rearrange("p a (q t w) -> p a t q w", t=SLOTS, w=2),
+            )
+
         round_wa(0)
         round_wa(1)
+        nc.tensor.transpose(bias_bank[:], bias_rows[:], identity[:])
+        nc.scalar.copy(biases[:], bias_bank[:, 0:8])
         round_wa(2)
         quantise_wa(0)
         gather_words(0, 0)
@@ -176,14 +177,6 @@ def tile_list_contact_gated_update_kernel(
             for t in range(SLOTS):
                 a_pass(0, t, half)
         quantise_wa(1)
-        nc.vector.tensor_copy(
-            wb_codes[:].rearrange("p a (t q w) -> p a t q w", t=SLOTS, w=4),
-            wbw_raw[:].rearrange("p a (q t w) -> p a t q w", t=SLOTS, w=4),
-        )
-        nc.vector.tensor_copy(
-            wb_planes[:].rearrange("p a (t q w) -> p a t q w", t=SLOTS, w=2),
-            wbs_raw[:].rearrange("p a (q t w) -> p a t q w", t=SLOTS, w=2),
-        )
         gather_words(1, 0)
         gather_words(1, 1)
         for half in range(2):
@@ -209,22 +202,23 @@ def tile_list_contact_gated_update_kernel(
                     a_biased[:, t, half * HALF : (half + 1) * HALF],
                     a_banks[t, half][:],
                     IDENT,
-                    bias=ba_cols[t][:],
+                    bias=biases[:, t : t + 1],
                 )
             if t < SLOTS - 1:
                 gate(t, 0, HALF)
                 gate(t, HALF, HALF)
+            if t == 0:
+                reorder_wb()
 
-        b_banks = []
-        for c in range(S // BANK_TOKENS):
-            cols = slice(c * BANK_TOKENS, (c + 1) * BANK_TOKENS)
-            bank = psum.tile([P, SLOTS, BANK_TOKENS], F32, name="bank")
-            b_banks.append(bank)
+        b_sums = sb("b_sums", [P, SLOTS, S], F32)
+        for half in range(2):
+            cols = slice(half * HALF, (half + 1) * HALF)
             for t in range(SLOTS):
+                bank = psum.tile([P, HALF], F32, name="bank")
                 for a in range(PASSES):
                     plane = v_scales[:] if a == 0 else v_scales_low[:, a - 1, :]
                     nc.tensor.matmul_mx(
-                        out=bank[:, t, :],
+                        out=bank[:],
                         lhsT=wb_codes[:, a, 64 * t : 64 * (t + 1)].bitcast(U8).bitcast(FP4X4),
                         lhsT_scale=wb_planes[:, a, 32 * t : 32 * (t + 1)].bitcast(U8),
                         rhs=v_words[a][:, cols].bitcast(FP8X4),
@@ -232,6 +226,7 @@ def tile_list_contact_gated_update_kernel(
                         start=(a == 0),
                         stop=(a == PASSES - 1),
                     )
+                nc.scalar.copy(b_sums[:, t, cols], bank[:])
 
         result = sb("result", [P, OUT_TILES, S], F32)
         out_view = out.rearrange("(c p) j -> p c j", p=P)
@@ -246,15 +241,13 @@ def tile_list_contact_gated_update_kernel(
             scales[i] = sb(f"scales{i}", [P, width], U8)
             if i == 0:
                 nc.scalar.copy(h_bf[0][:, 0:N, :], wo_raw[:].rearrange("p t n -> p n t"))
-            for j in range(OUT_CHUNKS[i] // BANK_TOKENS):
-                first = starts[i] + j * BANK_TOKENS
-                local = lead + j * BANK_TOKENS
-                nc.vector.tensor_tensor(
-                    h_bf[i][:, local : local + BANK_TOKENS, :].rearrange("p (n i) t -> p n t i", i=2),
-                    b_banks[first // BANK_TOKENS][:].rearrange("p t (n i) -> p n t i", i=2),
-                    gated[:, :, first : first + BANK_TOKENS].rearrange("p t (n i) -> p n t i", i=2),
-                    MULT,
-                )
+            cols = slice(starts[i], starts[i] + OUT_CHUNKS[i])
+            nc.vector.tensor_tensor(
+                h_bf[i][:, lead:width, :].rearrange("p (n i) t -> p n t i", i=2),
+                b_sums[:, :, cols].rearrange("p t (n i) -> p n t i", i=2),
+                gated[:, :, cols].rearrange("p t (n i) -> p n t i", i=2),
+                MULT,
+            )
 
         def finish(i):
             lead = N if i == 0 else 0
@@ -265,13 +258,10 @@ def tile_list_contact_gated_update_kernel(
                 scales=scales[i][:],
                 in_=h_bf[i][:].rearrange("p n t -> p (n t)"),
             )
-            per_bank = 512 // count
-            bank = None
             for c in range(OUT_TILES):
-                if c % per_bank == 0:
-                    bank = psum.tile([P, per_bank, count], F32, name="bank")
+                bank = psum.tile([P, count], F32, name="bank")
                 nc.tensor.matmul_mx(
-                    out=bank[:, c % per_bank, :],
+                    out=bank[:],
                     lhsT=codes[0][:, c * P : (c + 1) * P].bitcast(FP8X4),
                     lhsT_scale=scales[0][:, c * P : (c + 1) * P],
                     rhs=codes[i][:, lead : lead + count].bitcast(FP8X4),
@@ -280,7 +270,7 @@ def tile_list_contact_gated_update_kernel(
                     stop=True,
                 )
                 nc.scalar.activation(
-                    result[:, c, cols], bank[:, c % per_bank, :], IDENT, bias=bo_cols[:, c : c + 1]
+                    result[:, c, cols], bank[:], IDENT, bias=biases[:, SLOTS + c : SLOTS + c + 1]
                 )
             nc.sync.dma_start(out_view[:, :, cols], result[:, :, cols])
 

@@ -1,7 +1,6 @@
 from contextlib import ExitStack
 
 import concourse.mybir as mybir
-from concourse.masks import make_identity
 
 K, H, N, T, S = 1536, 512, 384, 2048, 1024
 FLOPS = 2 * S * (2 * K * H + H * N)
@@ -45,23 +44,20 @@ def tile_list_contact_gated_update_kernel(
 
         scale_win = sb("scale_win", [P, T // 4], I32)
         wbs_raw = sb("wbs_raw", [P, PASSES, H // 4], I32)
-        bias_rows = sb("bias_rows", [P, P], F32)
-        identity = sb("identity", [P, P], F32)
+        ba_cols = sb("ba_cols", [P, SLOTS], F32)
+        bo_cols = sb("bo_cols", [P, OUT_TILES], F32)
         v_scales = sb("v_scales", [P, S // 4], I32)
         v_scales_low = sb("v_scales_low", [P, PASSES - 1, S // 4], I32)
-        nc.gpsimd.memset(scale_win[:], 0)
-        nc.vector.memset(bias_rows[:], 0.0)
+        nc.vector.memset(scale_win[:], 0)
         nc.vector.memset(wbs_raw[:], 0)
         nc.vector.memset(v_scales_low[:], 0)
-        make_identity(nc, identity[:])
 
         wa_raw = [sb(f"wa_raw{a}", [P, SLOTS, H], F32) for a in range(PASSES)]
         tab = [sb(f"tab{a}", [P, T], I32) for a in range(PASSES)]
         wbw_raw = sb("wbw_raw", [P, PASSES, H // 2], I32)
         gates = [sb(f"gates{t}", [P, T], F32) for t in range(SLOTS)]
         wo_raw = sb("wo_raw", [P, SLOTS, N], F32)
-        g_view = gT.rearrange("(q t u) c -> t q u c", t=SLOTS, u=8)
-        wo_view = wo.rearrange("(q t u) n -> t q u n", t=SLOTS, u=8)
+        g_view = gT.rearrange("(p t) c -> t p c", t=SLOTS)
 
         def load_wa(a):
             nc.sync.dma_start(
@@ -71,42 +67,48 @@ def tile_list_contact_gated_update_kernel(
         def load_tab(a):
             nc.sync.dma_start(tab[a][:], tab_words[a].rearrange("p t i -> p (t i)").bitcast(I32))
 
-        load_wa(0)
-        load_wa(1)
-        for quad in range(4):
+        def load_tab_scales(quad):
             nc.sync.dma_start(
                 scale_win[32 * quad : 32 * quad + 4 * PASSES, :],
                 tab_scales[:, 4 * quad : 4 * quad + 4, :].bitcast(I32),
             )
-        nc.sync.dma_start(
-            bias_rows[0:SLOTS, :].rearrange("t (q u) -> t q u", u=8),
-            ba.rearrange("(q t u) -> t q u", t=SLOTS, u=8),
-        )
-        nc.sync.dma_start(
-            bias_rows[SLOTS : SLOTS + OUT_TILES, :], bo.rearrange("(c p) -> c p", p=P)
-        )
+
+        def load_wb_scales(quad):
+            nc.sync.dma_start(
+                wbs_raw[32 * quad : 32 * quad + 4, :, :],
+                wb_scales[:, 4 * quad : 4 * quad + 4, :].bitcast(I32).rearrange("a r c -> r a c"),
+            )
+
+        def lower_plane(a):
+            nc.sync.dma_start(v_scales_low[0:112, a - 1, :], v_scales[4 * a : 4 * a + 112, :])
+
+        nc.gpsimd.dma_start(ba_cols[:], ba.rearrange("(p t) -> p t", t=SLOTS))
+        nc.gpsimd.dma_start(bo_cols[:], bo.rearrange("(p c) -> p c", c=OUT_TILES))
+        nc.sync.dma_start(wbw_raw[:], wb_words.bitcast(I32).rearrange("a p c -> p a c"))
+        load_wa(0)
+        load_tab_scales(0)
+        load_tab_scales(1)
+        load_wa(1)
+        load_tab_scales(2)
+        load_tab_scales(3)
         load_tab(0)
+        load_wb_scales(0)
+        load_wb_scales(1)
         load_wa(2)
+        load_wb_scales(2)
+        load_wb_scales(3)
         load_tab(1)
         load_tab(2)
 
         nc.vector.tensor_copy(
             v_scales[:].bitcast(U8), scale_win[:].bitcast(U8).indirect(offsets[:])
         )
-
+        lower_plane(1)
         nc.sync.dma_start(gates[0][:], g_view[0])
-        for quad in range(4):
-            nc.sync.dma_start(
-                wbs_raw[32 * quad : 32 * quad + 4, :, :],
-                wb_scales[:, 4 * quad : 4 * quad + 4, :].bitcast(I32).rearrange("a r c -> r a c"),
-            )
-        nc.sync.dma_start(wbw_raw[:], wb_words.bitcast(I32).rearrange("a p c -> p a c"))
-        for a in range(1, PASSES):
-            nc.sync.dma_start(v_scales_low[0:112, a - 1, :], v_scales[4 * a : 4 * a + 112, :])
+        lower_plane(2)
         for t in range(1, SLOTS):
             nc.sync.dma_start(gates[t][:], g_view[t])
-        for t in range(SLOTS):
-            nc.sync.dma_start(wo_raw[:, t, :], wo_view[t])
+        nc.sync.dma_start(wo_raw[:], wo.rearrange("(p t) n -> p t n", t=SLOTS))
 
         wa_bf = [sb(f"wa_bf{a}", [P, SLOTS, P * 4], BF16) for a in range(PASSES)]
         wa_codes = [sb(f"wa_codes{a}", [P, H], U32) for a in range(PASSES)]
@@ -114,11 +116,10 @@ def tile_list_contact_gated_update_kernel(
         v_words = [sb(f"v_words{a}", [P, S], U32) for a in range(PASSES)]
 
         def round_wa(a):
-            src = wa_raw[a][:].rearrange("p j (q t u) -> p t q u j", t=SLOTS, u=8)
-            for t in range(SLOTS):
-                nc.scalar.copy(
-                    wa_bf[a][:, t, :].rearrange("p (q u j) -> p q u j", u=8, j=4), src[:, t]
-                )
+            src = wa_raw[a][:].rearrange("p j (m t) -> p m t j", t=SLOTS)
+            dst = wa_bf[a][:].rearrange("p t (m j) -> p m t j", j=4)
+            for t in range(0, SLOTS, 2):
+                nc.scalar.copy(dst[:, :, t : t + 2, :], src[:, :, t : t + 2, :])
 
         def quantise_wa(a):
             nc.vector.quantize_mx(
@@ -133,8 +134,6 @@ def tile_list_contact_gated_update_kernel(
                 tab[a][:].bitcast(U32).indirect(picks(half * HALF, HALF)),
             )
 
-        bias_bank = psum.tile([P, P], F32, name="bank")
-        biases = sb("biases", [P, 8], F32)
         a_banks = {}
         for t in range(SLOTS):
             for half in range(2):
@@ -157,34 +156,21 @@ def tile_list_contact_gated_update_kernel(
 
         def reorder_wb():
             nc.vector.tensor_copy(
-                wb_codes[:].rearrange("p a (t q w) -> p a t q w", t=SLOTS, w=4),
-                wbw_raw[:].rearrange("p a (q t w) -> p a t q w", t=SLOTS, w=4),
+                wb_codes[:].bitcast(U16).rearrange("p a (t m) -> p a t m", t=SLOTS),
+                wbw_raw[:].bitcast(U16).rearrange("p a (m t) -> p a t m", t=SLOTS),
             )
             nc.vector.tensor_copy(
-                wb_planes[:].rearrange("p a (t q w) -> p a t q w", t=SLOTS, w=2),
-                wbs_raw[:].rearrange("p a (q t w) -> p a t q w", t=SLOTS, w=2),
+                wb_planes[:].bitcast(U8).rearrange("p a (t m) -> p a t m", t=SLOTS),
+                wbs_raw[:].bitcast(U8).rearrange("p a (m t) -> p a t m", t=SLOTS),
             )
 
-        round_wa(0)
-        round_wa(1)
-        nc.tensor.transpose(bias_bank[:], bias_rows[:], identity[:])
-        nc.scalar.copy(biases[:], bias_bank[:, 0:8])
-        round_wa(2)
-        quantise_wa(0)
-        gather_words(0, 0)
-        gather_words(0, 1)
-        for half in range(2):
-            for t in range(SLOTS):
-                a_pass(0, t, half)
-        quantise_wa(1)
-        gather_words(1, 0)
-        gather_words(1, 1)
-        for half in range(2):
-            for t in range(SLOTS):
-                a_pass(1, t, half)
-        quantise_wa(2)
-        gather_words(2, 0)
-        gather_words(2, 1)
+        for a in range(PASSES):
+            round_wa(a)
+            quantise_wa(a)
+            gather_words(a, 0)
+            gather_words(a, 1)
+            if a == 0:
+                reorder_wb()
 
         a_biased = sb("a_biased", [P, SLOTS, S], F32)
         gated = sb("gated", [P, SLOTS, S], F32)
@@ -197,18 +183,19 @@ def tile_list_contact_gated_update_kernel(
 
         for t in range(SLOTS):
             for half in range(2):
-                a_pass(PASSES - 1, t, half)
+                for a in range(PASSES):
+                    a_pass(a, t, half)
                 nc.scalar.activation(
                     a_biased[:, t, half * HALF : (half + 1) * HALF],
                     a_banks[t, half][:],
                     IDENT,
-                    bias=biases[:, t : t + 1],
+                    bias=ba_cols[:, t : t + 1],
                 )
-            if t < SLOTS - 1:
+            if t == 0:
                 gate(t, 0, HALF)
                 gate(t, HALF, HALF)
-            if t == 0:
-                reorder_wb()
+            elif t < SLOTS - 1:
+                gate(t, 0, S)
 
         b_sums = sb("b_sums", [P, SLOTS, S], F32)
         for half in range(2):
@@ -229,7 +216,7 @@ def tile_list_contact_gated_update_kernel(
                 nc.scalar.copy(b_sums[:, t, cols], bank[:])
 
         result = sb("result", [P, OUT_TILES, S], F32)
-        out_view = out.rearrange("(c p) j -> p c j", p=P)
+        out_view = out.rearrange("(p c) j -> p c j", c=OUT_TILES)
         starts = [sum(OUT_CHUNKS[:i]) for i in range(len(OUT_CHUNKS))]
         h_bf, codes, scales = {}, {}, {}
 
@@ -240,7 +227,10 @@ def tile_list_contact_gated_update_kernel(
             codes[i] = sb(f"codes{i}", [P, width], U32)
             scales[i] = sb(f"scales{i}", [P, width], U8)
             if i == 0:
-                nc.scalar.copy(h_bf[0][:, 0:N, :], wo_raw[:].rearrange("p t n -> p n t"))
+                nc.scalar.copy(
+                    h_bf[0][:, 0:N, :].rearrange("p (c m) t -> p m c t", c=OUT_TILES),
+                    wo_raw[:].rearrange("p t (m c) -> p m c t", c=OUT_TILES),
+                )
             cols = slice(starts[i], starts[i] + OUT_CHUNKS[i])
             nc.vector.tensor_tensor(
                 h_bf[i][:, lead:width, :].rearrange("p (n i) t -> p n t i", i=2),
@@ -269,9 +259,12 @@ def tile_list_contact_gated_update_kernel(
                     start=True,
                     stop=True,
                 )
-                nc.scalar.activation(
-                    result[:, c, cols], bank[:], IDENT, bias=biases[:, SLOTS + c : SLOTS + c + 1]
-                )
+                if i == len(OUT_CHUNKS) - 1 and c == 1:
+                    nc.vector.tensor_scalar_add(result[:, c, cols], bank[:], bo_cols[:, c : c + 1])
+                else:
+                    nc.scalar.activation(
+                        result[:, c, cols], bank[:], IDENT, bias=bo_cols[:, c : c + 1]
+                    )
             nc.sync.dma_start(out_view[:, :, cols], result[:, :, cols])
 
         for first in range(0, S, 256):

@@ -156,12 +156,12 @@ def tile_list_contact_gated_update_kernel(
 
         def reorder_wb():
             nc.vector.tensor_copy(
-                wb_codes[:].bitcast(U16).rearrange("p a (t m) -> p a t m", t=SLOTS),
-                wbw_raw[:].bitcast(U16).rearrange("p a (m t) -> p a t m", t=SLOTS),
+                wb_codes[:].bitcast(U16).rearrange("p a (t m) -> p t a m", t=SLOTS),
+                wbw_raw[:].bitcast(U16).rearrange("p a (m t) -> p t a m", t=SLOTS),
             )
             nc.vector.tensor_copy(
-                wb_planes[:].bitcast(U8).rearrange("p a (t m) -> p a t m", t=SLOTS),
-                wbs_raw[:].bitcast(U8).rearrange("p a (m t) -> p a t m", t=SLOTS),
+                wb_planes[:].bitcast(U8).rearrange("p a (t m) -> p t a m", t=SLOTS),
+                wbs_raw[:].bitcast(U8).rearrange("p a (m t) -> p t a m", t=SLOTS),
             )
 
         for a in range(PASSES):
@@ -233,9 +233,9 @@ def tile_list_contact_gated_update_kernel(
                 )
             cols = slice(starts[i], starts[i] + OUT_CHUNKS[i])
             nc.vector.tensor_tensor(
-                h_bf[i][:, lead:width, :].rearrange("p (n i) t -> p n t i", i=2),
-                b_sums[:, :, cols].rearrange("p t (n i) -> p n t i", i=2),
-                gated[:, :, cols].rearrange("p t (n i) -> p n t i", i=2),
+                h_bf[i][:, lead:width, :].rearrange("p (n i) t -> p n t i", i=4),
+                b_sums[:, :, cols].rearrange("p t (n i) -> p n t i", i=4),
+                gated[:, :, cols].rearrange("p t (n i) -> p n t i", i=4),
                 MULT,
             )
 

@@ -116,10 +116,11 @@ def tile_list_contact_gated_update_kernel(
         v_words = [sb(f"v_words{a}", [P, S], U32) for a in range(PASSES)]
 
         def round_wa(a):
-            src = wa_raw[a][:].rearrange("p j (m t) -> p m t j", t=SLOTS)
-            dst = wa_bf[a][:].rearrange("p t (m j) -> p m t j", j=4)
+            src = wa_raw[a][:].rearrange("p j (m t) -> p m j t", t=SLOTS)
+            dst = wa_bf[a][:].rearrange("p t (m j) -> p m j t", j=4)
+            copy = nc.vector.tensor_copy if a == 0 else nc.scalar.copy
             for t in range(0, SLOTS, 2):
-                nc.scalar.copy(dst[:, :, t : t + 2, :], src[:, :, t : t + 2, :])
+                copy(dst[:, :, :, t : t + 2], src[:, :, :, t : t + 2])
 
         def quantise_wa(a):
             nc.vector.quantize_mx(

@@ -83,7 +83,8 @@ def tile_list_contact_gated_update_kernel(
             nc.sync.dma_start(v_scales_low[0:112, a - 1, :], v_scales[4 * a : 4 * a + 112, :])
 
         nc.gpsimd.dma_start(ba_cols[:], ba.rearrange("(p t) -> p t", t=SLOTS))
-        nc.gpsimd.dma_start(bo_cols[:], bo.rearrange("(p c) -> p c", c=OUT_TILES))
+        with nc.allow_non_contiguous_dma(reason="one bias value for each partition"):
+            nc.gpsimd.dma_start(bo_cols[:], bo.rearrange("(c p) -> p c", p=P))
         nc.sync.dma_start(wbw_raw[:], wb_words.bitcast(I32).rearrange("a p c -> p a c"))
         load_wa(0)
         load_tab_scales(0)
@@ -217,7 +218,7 @@ def tile_list_contact_gated_update_kernel(
                 nc.scalar.copy(b_sums[:, t, cols], bank[:])
 
         result = sb("result", [P, OUT_TILES, S], F32)
-        out_view = out.rearrange("(p c) j -> p c j", c=OUT_TILES)
+        out_view = out.rearrange("(c p) j -> p c j", p=P)
         starts = [sum(OUT_CHUNKS[:i]) for i in range(len(OUT_CHUNKS))]
         h_bf, codes, scales = {}, {}, {}
 
@@ -229,8 +230,8 @@ def tile_list_contact_gated_update_kernel(
             scales[i] = sb(f"scales{i}", [P, width], U8)
             if i == 0:
                 nc.scalar.copy(
-                    h_bf[0][:, 0:N, :].rearrange("p (c m) t -> p m c t", c=OUT_TILES),
-                    wo_raw[:].rearrange("p t (m c) -> p m c t", c=OUT_TILES),
+                    h_bf[0][:, 0:N, :].rearrange("p (n i) t -> p n t i", i=4),
+                    wo_raw[:].rearrange("p t (n i) -> p n t i", i=4),
                 )
             cols = slice(starts[i], starts[i] + OUT_CHUNKS[i])
             nc.vector.tensor_tensor(

@@ -105,11 +105,11 @@ def tile_list_contact_gated_update_kernel(
             v_scales[:].bitcast(U8), scale_win[:].bitcast(U8).indirect(offsets[:])
         )
         lower_plane(1)
+        nc.sync.dma_start(wo_raw[:], wo.rearrange("(p t) n -> p t n", t=SLOTS))
         nc.sync.dma_start(gates[0][:], g_view[0])
         lower_plane(2)
         for t in range(1, SLOTS):
             nc.sync.dma_start(gates[t][:], g_view[t])
-        nc.sync.dma_start(wo_raw[:], wo.rearrange("(p t) n -> p t n", t=SLOTS))
 
         wa_bf = [sb(f"wa_bf{a}", [P, SLOTS, P * 4], BF16) for a in range(PASSES)]
         wa_codes = [sb(f"wa_codes{a}", [P, H], U32) for a in range(PASSES)]
@@ -199,23 +199,29 @@ def tile_list_contact_gated_update_kernel(
             elif t < SLOTS - 1:
                 gate(t, 0, S)
 
-        b_sums = sb("b_sums", [P, SLOTS, S], F32)
-        for half in range(2):
-            cols = slice(half * HALF, (half + 1) * HALF)
+        def b_group(target, t, cols):
+            for a in range(PASSES):
+                plane = v_scales[:] if a == 0 else v_scales_low[:, a - 1, :]
+                nc.tensor.matmul_mx(
+                    out=target,
+                    lhsT=wb_codes[:, a, 64 * t : 64 * (t + 1)].bitcast(U8).bitcast(FP4X4),
+                    lhsT_scale=wb_planes[:, a, 32 * t : 32 * (t + 1)].bitcast(U8),
+                    rhs=v_words[a][:, cols].bitcast(FP8X4),
+                    rhs_scale=plane.bitcast(U8)[:, cols],
+                    start=(a == 0),
+                    stop=(a == PASSES - 1),
+                )
+
+        b_sums = sb("b_sums", [P, SLOTS, HALF], F32)
+        for t in range(SLOTS):
+            bank = psum.tile([P, HALF], F32, name="bank")
+            b_group(bank[:], t, slice(0, HALF))
+            nc.scalar.copy(b_sums[:, t, :], bank[:])
+        b_blocks = {}
+        for first in range(HALF, S, P):
+            b_blocks[first] = psum.tile([P, SLOTS, P], F32, name="bank")
             for t in range(SLOTS):
-                bank = psum.tile([P, HALF], F32, name="bank")
-                for a in range(PASSES):
-                    plane = v_scales[:] if a == 0 else v_scales_low[:, a - 1, :]
-                    nc.tensor.matmul_mx(
-                        out=bank[:],
-                        lhsT=wb_codes[:, a, 64 * t : 64 * (t + 1)].bitcast(U8).bitcast(FP4X4),
-                        lhsT_scale=wb_planes[:, a, 32 * t : 32 * (t + 1)].bitcast(U8),
-                        rhs=v_words[a][:, cols].bitcast(FP8X4),
-                        rhs_scale=plane.bitcast(U8)[:, cols],
-                        start=(a == 0),
-                        stop=(a == PASSES - 1),
-                    )
-                nc.scalar.copy(b_sums[:, t, cols], bank[:])
+                b_group(b_blocks[first][:, t, :], t, slice(first, first + P))
 
         result = sb("result", [P, OUT_TILES, S], F32)
         out_view = out.rearrange("(c p) j -> p c j", p=P)
@@ -233,13 +239,18 @@ def tile_list_contact_gated_update_kernel(
                     h_bf[0][:, 0:N, :].rearrange("p (n i) t -> p n t i", i=4),
                     wo_raw[:].rearrange("p t (n i) -> p n t i", i=4),
                 )
-            cols = slice(starts[i], starts[i] + OUT_CHUNKS[i])
-            nc.vector.tensor_tensor(
-                h_bf[i][:, lead:width, :].rearrange("p (n i) t -> p n t i", i=4),
-                b_sums[:, :, cols].rearrange("p t (n i) -> p n t i", i=4),
-                gated[:, :, cols].rearrange("p t (n i) -> p n t i", i=4),
-                MULT,
-            )
+            start, end = starts[i], starts[i] + OUT_CHUNKS[i]
+            pieces = [(start, min(end, HALF))] if start < HALF else []
+            pieces.extend((first, first + P) for first in range(max(start, HALF), end, P))
+            for first, last in pieces:
+                b_part = b_sums[:, :, first:last] if first < HALF else b_blocks[first][:]
+                shift = lead - start
+                nc.vector.tensor_tensor(
+                    h_bf[i][:, first + shift : last + shift, :].rearrange("p (n i) t -> p n t i", i=4),
+                    b_part.rearrange("p t (n i) -> p n t i", i=4),
+                    gated[:, :, first:last].rearrange("p t (n i) -> p n t i", i=4),
+                    MULT,
+                )
 
         def finish(i):
             lead = N if i == 0 else 0

@@ -105,9 +105,9 @@ def tile_list_contact_gated_update_kernel(
             v_scales[:].bitcast(U8), scale_win[:].bitcast(U8).indirect(offsets[:])
         )
         lower_plane(1)
-        nc.sync.dma_start(wo_raw[:], wo.rearrange("(p t) n -> p t n", t=SLOTS))
         nc.sync.dma_start(gates[0][:], g_view[0])
         lower_plane(2)
+        nc.sync.dma_start(wo_raw[:], wo.rearrange("(p t) n -> p t n", t=SLOTS))
         for t in range(1, SLOTS):
             nc.sync.dma_start(gates[t][:], g_view[t])
 
@@ -119,8 +119,8 @@ def tile_list_contact_gated_update_kernel(
         def round_wa(a):
             src = wa_raw[a][:].rearrange("p j (m t) -> p m j t", t=SLOTS)
             dst = wa_bf[a][:].rearrange("p t (m j) -> p m j t", j=4)
-            copy = nc.vector.tensor_copy if a == 0 else nc.scalar.copy
             for t in range(0, SLOTS, 2):
+                copy = nc.vector.tensor_copy if a == 0 or (a == 1 and t == 0) else nc.scalar.copy
                 copy(dst[:, :, :, t : t + 2], src[:, :, :, t : t + 2])
 
         def quantise_wa(a):

@@ -21,7 +21,8 @@ PASSES = K // 512
 SLOTS = 4
 HALF = 512
 OUT_TILES = N // P
-OUT_CHUNKS = [128, 256, 256, 256, 128]
+OUT_CHUNKS = [128, 256, 128, 256, 128, 128]
+WO_CHUNK = 0
 
 
 def tile_list_contact_gated_update_kernel(
@@ -30,11 +31,11 @@ def tile_list_contact_gated_update_kernel(
     nc = tc.nc
     with ExitStack() as ctx:
         keep = ctx.enter_context(tc.tile_pool(name="keep", bufs=1))
-        ring = ctx.enter_context(tc.tile_pool(name="ring", bufs=2))
-        psum = ctx.enter_context(tc.psum_pool(name="psum", bufs=8))
+        psum = ctx.enter_context(tc.psum_pool(name="psum", bufs=4))
+        psum_b = ctx.enter_context(tc.psum_pool(name="psum_b", bufs=4))
 
-        def sb(name, shape, dtype):
-            return keep.tile(shape, dtype, name=name, align_bytes=64)
+        def sb(name, shape, dtype, tag=None):
+            return keep.tile(shape, dtype, name=name, tag=tag or name, align_bytes=64)
 
         offsets = keep.tile([P, S // 16], U16, name="offsets")
         nc.sync.dma_start(offsets[:], offs)
@@ -48,7 +49,7 @@ def tile_list_contact_gated_update_kernel(
         bo_cols = sb("bo_cols", [P, OUT_TILES], F32)
         v_scales = sb("v_scales", [P, S // 4], I32)
         v_scales_low = sb("v_scales_low", [P, PASSES - 1, S // 4], I32)
-        nc.vector.memset(scale_win[:], 0)
+        nc.gpsimd.memset(scale_win[:], 0)
         nc.vector.memset(wbs_raw[:], 0)
         nc.vector.memset(v_scales_low[:], 0)
 
@@ -83,44 +84,42 @@ def tile_list_contact_gated_update_kernel(
             nc.sync.dma_start(v_scales_low[0:112, a - 1, :], v_scales[4 * a : 4 * a + 112, :])
 
         nc.gpsimd.dma_start(ba_cols[:], ba.rearrange("(p t) -> p t", t=SLOTS))
-        with nc.allow_non_contiguous_dma(reason="one bias value for each partition"):
-            nc.gpsimd.dma_start(bo_cols[:], bo.rearrange("(c p) -> p c", p=P))
         nc.sync.dma_start(wbw_raw[:], wb_words.bitcast(I32).rearrange("a p c -> p a c"))
         load_wa(0)
-        load_tab_scales(0)
-        load_tab_scales(1)
+        for quad in range(4):
+            load_tab_scales(quad)
         load_wa(1)
-        load_tab_scales(2)
-        load_tab_scales(3)
         load_tab(0)
-        load_wb_scales(0)
-        load_wb_scales(1)
-        load_wa(2)
-        load_wb_scales(2)
-        load_wb_scales(3)
+        for quad in range(4):
+            load_wb_scales(quad)
         load_tab(1)
+        load_wa(2)
         load_tab(2)
 
         nc.vector.tensor_copy(
             v_scales[:].bitcast(U8), scale_win[:].bitcast(U8).indirect(offsets[:])
         )
-        lower_plane(1)
         nc.sync.dma_start(gates[0][:], g_view[0])
+        lower_plane(1)
         lower_plane(2)
-        nc.sync.dma_start(wo_raw[:], wo.rearrange("(p t) n -> p t n", t=SLOTS))
         for t in range(1, SLOTS):
             nc.sync.dma_start(gates[t][:], g_view[t])
+        nc.sync.dma_start(wo_raw[:], wo.rearrange("(p t) n -> p t n", t=SLOTS))
+        with nc.allow_non_contiguous_dma(reason="one bias value for each partition"):
+            nc.sync.dma_start(bo_cols[:], bo.rearrange("(c p) -> p c", p=P))
 
         wa_bf = [sb(f"wa_bf{a}", [P, SLOTS, P * 4], BF16) for a in range(PASSES)]
         wa_codes = [sb(f"wa_codes{a}", [P, H], U32) for a in range(PASSES)]
         wa_scales = [sb(f"wa_scales{a}", [P, H], U8) for a in range(PASSES)]
-        v_words = [sb(f"v_words{a}", [P, S], U32) for a in range(PASSES)]
+        v_words = {
+            (a, half): sb(f"v_words{a}{half}", [P, HALF], U32) for a in range(PASSES) for half in range(2)
+        }
 
         def round_wa(a):
             src = wa_raw[a][:].rearrange("p j (m t) -> p m j t", t=SLOTS)
             dst = wa_bf[a][:].rearrange("p t (m j) -> p m j t", j=4)
             for t in range(0, SLOTS, 2):
-                copy = nc.vector.tensor_copy if a == 0 or (a == 1 and t == 0) else nc.scalar.copy
+                copy = nc.vector.tensor_copy if a == 0 or t == 0 else nc.scalar.copy
                 copy(dst[:, :, :, t : t + 2], src[:, :, :, t : t + 2])
 
         def quantise_wa(a):
@@ -130,11 +129,11 @@ def tile_list_contact_gated_update_kernel(
                 in_=wa_bf[a][:].rearrange("p t c -> p (t c)"),
             )
 
-        def gather_words(a, half):
-            nc.vector.tensor_copy(
-                v_words[a][:, half * HALF : (half + 1) * HALF],
-                tab[a][:].bitcast(U32).indirect(picks(half * HALF, HALF)),
-            )
+        def gather_words(a):
+            for half in range(2):
+                nc.vector.tensor_copy(
+                    v_words[a, half][:], tab[a][:].bitcast(U32).indirect(picks(half * HALF, HALF))
+                )
 
         a_banks = {}
         for t in range(SLOTS):
@@ -147,7 +146,7 @@ def tile_list_contact_gated_update_kernel(
                 out=a_banks[t, half][:],
                 lhsT=wa_codes[a][:, t * P : (t + 1) * P].bitcast(FP8X4),
                 lhsT_scale=wa_scales[a][:, t * P : (t + 1) * P],
-                rhs=v_words[a][:, cols].bitcast(FP8X4),
+                rhs=v_words[a, half][:].bitcast(FP8X4),
                 rhs_scale=v_scales[4 * a : P, :].bitcast(U8)[:, cols],
                 start=(a == 0),
                 stop=(a == PASSES - 1),
@@ -166,13 +165,15 @@ def tile_list_contact_gated_update_kernel(
                 wbs_raw[:].bitcast(U8).rearrange("p a (m t) -> p t a m", t=SLOTS),
             )
 
-        for a in range(PASSES):
+        reorder_wb()
+        for a in range(2):
             round_wa(a)
             quantise_wa(a)
-            gather_words(a, 0)
-            gather_words(a, 1)
-            if a == 0:
-                reorder_wb()
+        gather_words(0)
+        gather_words(1)
+        round_wa(2)
+        quantise_wa(2)
+        gather_words(2)
 
         a_biased = sb("a_biased", [P, SLOTS, S], F32)
         gated = sb("gated", [P, SLOTS, S], F32)
@@ -200,26 +201,26 @@ def tile_list_contact_gated_update_kernel(
                 gate(t, 0, S)
 
         def b_group(target, t, cols):
-            for a in range(PASSES):
+            for a in reversed(range(PASSES)):
                 plane = v_scales[:] if a == 0 else v_scales_low[:, a - 1, :]
                 nc.tensor.matmul_mx(
                     out=target,
                     lhsT=wb_codes[:, a, 64 * t : 64 * (t + 1)].bitcast(U8).bitcast(FP4X4),
                     lhsT_scale=wb_planes[:, a, 32 * t : 32 * (t + 1)].bitcast(U8),
-                    rhs=v_words[a][:, cols].bitcast(FP8X4),
+                    rhs=v_words[a, cols.start // HALF][:, cols.start % HALF : (cols.stop - 1) % HALF + 1].bitcast(FP8X4),
                     rhs_scale=plane.bitcast(U8)[:, cols],
-                    start=(a == 0),
-                    stop=(a == PASSES - 1),
+                    start=(a == PASSES - 1),
+                    stop=(a == 0),
                 )
 
         b_sums = sb("b_sums", [P, SLOTS, HALF], F32)
         for t in range(SLOTS):
-            bank = psum.tile([P, HALF], F32, name="bank")
+            bank = psum_b.tile([P, HALF], F32, name="bank")
             b_group(bank[:], t, slice(0, HALF))
             nc.scalar.copy(b_sums[:, t, :], bank[:])
         b_blocks = {}
         for first in range(HALF, S, P):
-            b_blocks[first] = psum.tile([P, SLOTS, P], F32, name="bank")
+            b_blocks[first] = psum_b.tile([P, SLOTS, P], F32, name="bank")
             for t in range(SLOTS):
                 b_group(b_blocks[first][:, t, :], t, slice(first, first + P))
 
@@ -229,14 +230,14 @@ def tile_list_contact_gated_update_kernel(
         h_bf, codes, scales = {}, {}, {}
 
         def make_h(i):
-            lead = N if i == 0 else 0
+            lead = N if i == WO_CHUNK else 0
             width = lead + OUT_CHUNKS[i]
-            h_bf[i] = ring.tile([P, width, SLOTS], BF16, name="h_bf", align_bytes=64)
+            h_bf[i] = sb(f"h_bf{i}", [P, width, SLOTS], BF16, tag="h_bf0" if i == 2 else None)
             codes[i] = sb(f"codes{i}", [P, width], U32)
             scales[i] = sb(f"scales{i}", [P, width], U8)
-            if i == 0:
+            if i == WO_CHUNK:
                 nc.scalar.copy(
-                    h_bf[0][:, 0:N, :].rearrange("p (n i) t -> p n t i", i=4),
+                    h_bf[i][:, 0:N, :].rearrange("p (n i) t -> p n t i", i=4),
                     wo_raw[:].rearrange("p t (n i) -> p n t i", i=4),
                 )
             start, end = starts[i], starts[i] + OUT_CHUNKS[i]
@@ -252,21 +253,23 @@ def tile_list_contact_gated_update_kernel(
                     MULT,
                 )
 
-        def finish(i):
-            lead = N if i == 0 else 0
-            count = OUT_CHUNKS[i]
-            cols = slice(starts[i], starts[i] + count)
+        def quantise_h(i):
             nc.vector.quantize_mx(
                 out=codes[i][:].bitcast(FP8X4),
                 scales=scales[i][:],
                 in_=h_bf[i][:].rearrange("p n t -> p (n t)"),
             )
+
+        def finish(i):
+            lead = N if i == WO_CHUNK else 0
+            count = OUT_CHUNKS[i]
+            cols = slice(starts[i], starts[i] + count)
             for c in range(OUT_TILES):
                 bank = psum.tile([P, count], F32, name="bank")
                 nc.tensor.matmul_mx(
                     out=bank[:],
-                    lhsT=codes[0][:, c * P : (c + 1) * P].bitcast(FP8X4),
-                    lhsT_scale=scales[0][:, c * P : (c + 1) * P],
+                    lhsT=codes[WO_CHUNK][:, c * P : (c + 1) * P].bitcast(FP8X4),
+                    lhsT_scale=scales[WO_CHUNK][:, c * P : (c + 1) * P],
                     rhs=codes[i][:, lead : lead + count].bitcast(FP8X4),
                     rhs_scale=scales[i][:, lead : lead + count],
                     start=True,
@@ -280,10 +283,16 @@ def tile_list_contact_gated_update_kernel(
                     )
             nc.sync.dma_start(out_view[:, :, cols], result[:, :, cols])
 
-        for first in range(0, S, 256):
-            gate(SLOTS - 1, first, 256)
-        for i in range(len(OUT_CHUNKS)):
-            make_h(i)
+        gate(SLOTS - 1, 0, HALF)
+        gate(SLOTS - 1, HALF, HALF)
+        last = len(OUT_CHUNKS) - 1
+        for i in range(last + 2):
+            if i <= last:
+                make_h(i)
             if i > 0:
-                finish(i - 1)
-        finish(len(OUT_CHUNKS) - 1)
+                quantise_h(i - 1)
+                if i - 1 == WO_CHUNK:
+                    for earlier in range(WO_CHUNK):
+                        finish(earlier)
+                if i - 1 >= WO_CHUNK:
+                    finish(i - 1)

@@ -89,12 +89,11 @@ def tile_list_contact_gated_update_kernel(
         for quad in range(4):
             load_tab_scales(quad)
         load_wa(1)
-        load_tab(0)
+        load_wa(2)
         for quad in range(4):
             load_wb_scales(quad)
-        load_tab(1)
-        load_wa(2)
-        load_tab(2)
+        for a in range(PASSES):
+            load_tab(a)
 
         nc.vector.tensor_copy(
             v_scales[:].bitcast(U8), scale_win[:].bitcast(U8).indirect(offsets[:])
@@ -119,7 +118,7 @@ def tile_list_contact_gated_update_kernel(
             src = wa_raw[a][:].rearrange("p j (m t) -> p m j t", t=SLOTS)
             dst = wa_bf[a][:].rearrange("p t (m j) -> p m j t", j=4)
             for t in range(0, SLOTS, 2):
-                copy = nc.vector.tensor_copy if a == 0 or t == 0 else nc.scalar.copy
+                copy = nc.vector.tensor_copy if a > 0 and t == 0 else nc.scalar.copy
                 copy(dst[:, :, :, t : t + 2], src[:, :, :, t : t + 2])
 
         def quantise_wa(a):
@@ -166,14 +165,11 @@ def tile_list_contact_gated_update_kernel(
             )
 
         reorder_wb()
-        for a in range(2):
+        for a in range(PASSES):
             round_wa(a)
             quantise_wa(a)
-        gather_words(0)
-        gather_words(1)
-        round_wa(2)
-        quantise_wa(2)
-        gather_words(2)
+        for a in range(PASSES):
+            gather_words(a)
 
         a_biased = sb("a_biased", [P, SLOTS, S], F32)
         gated = sb("gated", [P, SLOTS, S], F32)

@@ -74,16 +74,15 @@ def tile_list_contact_gated_update_kernel(
                 tab_scales[:, 4 * quad : 4 * quad + 4, :].bitcast(I32),
             )
 
-        def load_wb_scales(quad):
+        def load_wb_scales(row):
             nc.sync.dma_start(
-                wbs_raw[32 * quad : 32 * quad + 4, :, :],
-                wb_scales[:, 4 * quad : 4 * quad + 4, :].bitcast(I32).rearrange("a r c -> r a c"),
+                wbs_raw[row:P:32, :, :],
+                wb_scales[:, row:16:4, :].bitcast(I32).rearrange("a q c -> q a c"),
             )
 
         def lower_plane(a):
             nc.sync.dma_start(v_scales_low[0:112, a - 1, :], v_scales[4 * a : 4 * a + 112, :])
 
-        nc.gpsimd.dma_start(ba_cols[:], ba.rearrange("(p t) -> p t", t=SLOTS))
         nc.sync.dma_start(wbw_raw[:], wb_words.bitcast(I32).rearrange("a p c -> p a c"))
         load_wa(0)
         for quad in range(4):
@@ -98,6 +97,7 @@ def tile_list_contact_gated_update_kernel(
         nc.vector.tensor_copy(
             v_scales[:].bitcast(U8), scale_win[:].bitcast(U8).indirect(offsets[:])
         )
+        nc.sync.dma_start(ba_cols[:], ba.rearrange("(p t) -> p t", t=SLOTS))
         nc.sync.dma_start(gates[0][:], g_view[0])
         lower_plane(1)
         lower_plane(2)
@@ -238,9 +238,10 @@ def tile_list_contact_gated_update_kernel(
                 )
             start, end = starts[i], starts[i] + OUT_CHUNKS[i]
             pieces = [(start, min(end, HALF))] if start < HALF else []
-            pieces.extend((first, first + P) for first in range(max(start, HALF), end, P))
+            pieces.extend((first, min(first + P, end)) for first in range(max(start, HALF), end, P))
             for first, last in pieces:
-                b_part = b_sums[:, :, first:last] if first < HALF else b_blocks[first][:]
+                block = first - first % P
+                b_part = b_sums[:, :, first:last] if first < HALF else b_blocks[block][:, :, first - block : last - block]
                 shift = lead - start
                 nc.vector.tensor_tensor(
                     h_bf[i][:, first + shift : last + shift, :].rearrange("p (n i) t -> p n t i", i=4),
@@ -277,7 +278,8 @@ def tile_list_contact_gated_update_kernel(
                     nc.scalar.activation(
                         result[:, c, cols], bank[:], IDENT, bias=bo_cols[:, c : c + 1]
                     )
-            nc.sync.dma_start(out_view[:, :, cols], result[:, :, cols])
+            queue = nc.scalar if i == len(OUT_CHUNKS) - 1 else nc.sync
+            queue.dma_start(out_view[:, :, cols], result[:, :, cols])
 
         gate(SLOTS - 1, 0, HALF)
         gate(SLOTS - 1, HALF, HALF)

@@ -38,7 +38,6 @@ def tile_list_contact_gated_update_kernel(
             return keep.tile(shape, dtype, name=name, tag=tag or name, align_bytes=64)
 
         offsets = keep.tile([P, S // 16], U16, name="offsets")
-        nc.sync.dma_start(offsets[:], offs)
 
         def picks(first, count):
             return offsets[:, first // 16 : (first + count) // 16]
@@ -85,22 +84,24 @@ def tile_list_contact_gated_update_kernel(
 
         nc.sync.dma_start(wbw_raw[:], wb_words.bitcast(I32).rearrange("a p c -> p a c"))
         load_wa(0)
+        nc.sync.dma_start(offsets[:], offs)
         for quad in range(4):
             load_tab_scales(quad)
+        load_tab(0)
         load_wa(1)
         load_wa(2)
-        for quad in range(4):
-            load_wb_scales(quad)
-        for a in range(PASSES):
-            load_tab(a)
+        load_tab(1)
+        load_tab(2)
+        for row in range(4):
+            load_wb_scales(row)
 
         nc.vector.tensor_copy(
             v_scales[:].bitcast(U8), scale_win[:].bitcast(U8).indirect(offsets[:])
         )
         nc.sync.dma_start(ba_cols[:], ba.rearrange("(p t) -> p t", t=SLOTS))
-        nc.sync.dma_start(gates[0][:], g_view[0])
-        lower_plane(1)
         lower_plane(2)
+        lower_plane(1)
+        nc.sync.dma_start(gates[0][:], g_view[0])
         for t in range(1, SLOTS):
             nc.sync.dma_start(gates[t][:], g_view[t])
         nc.sync.dma_start(wo_raw[:], wo.rearrange("(p t) n -> p t n", t=SLOTS))
@@ -154,22 +155,27 @@ def tile_list_contact_gated_update_kernel(
         wb_codes = sb("wb_codes", [P, PASSES, H // 2], I32)
         wb_planes = sb("wb_planes", [P, PASSES, H // 4], I32)
 
-        def reorder_wb():
+        def reorder_wb_codes():
             nc.vector.tensor_copy(
                 wb_codes[:].bitcast(U16).rearrange("p a (t m) -> p t a m", t=SLOTS),
                 wbw_raw[:].bitcast(U16).rearrange("p a (m t) -> p t a m", t=SLOTS),
             )
+
+        def reorder_wb_planes():
             nc.vector.tensor_copy(
                 wb_planes[:].bitcast(U8).rearrange("p a (t m) -> p t a m", t=SLOTS),
                 wbs_raw[:].bitcast(U8).rearrange("p a (m t) -> p t a m", t=SLOTS),
             )
 
-        reorder_wb()
+        reorder_wb_codes()
         for a in range(PASSES):
             round_wa(a)
             quantise_wa(a)
-        for a in range(PASSES):
-            gather_words(a)
+            if a == 0:
+                gather_words(0)
+        gather_words(1)
+        gather_words(2)
+        reorder_wb_planes()
 
         a_biased = sb("a_biased", [P, SLOTS, S], F32)
         gated = sb("gated", [P, SLOTS, S], F32)
@@ -278,8 +284,11 @@ def tile_list_contact_gated_update_kernel(
                     nc.scalar.activation(
                         result[:, c, cols], bank[:], IDENT, bias=bo_cols[:, c : c + 1]
                     )
-            queue = nc.scalar if i == len(OUT_CHUNKS) - 1 else nc.sync
-            queue.dma_start(out_view[:, :, cols], result[:, :, cols])
+                if i == len(OUT_CHUNKS) - 1:
+                    queue = nc.sync if c == 1 else nc.scalar
+                    queue.dma_start(out_view[:, c, cols], result[:, c, cols])
+            if i < len(OUT_CHUNKS) - 1:
+                nc.sync.dma_start(out_view[:, :, cols], result[:, :, cols])
 
         gate(SLOTS - 1, 0, HALF)
         gate(SLOTS - 1, HALF, HALF)

@@ -268,7 +268,8 @@ def tile_list_contact_gated_update_kernel(
             count = OUT_CHUNKS[i]
             cols = slice(starts[i], starts[i] + count)
             for c in range(OUT_TILES):
-                bank = psum.tile([P, count], F32, name="bank")
+                pool = psum_b if i == last - 1 or (i == last and c == 0) else psum
+                bank = pool.tile([P, count], F32, name="bank")
                 nc.tensor.matmul_mx(
                     out=bank[:],
                     lhsT=codes[WO_CHUNK][:, c * P : (c + 1) * P].bitcast(FP8X4),
@@ -278,28 +279,28 @@ def tile_list_contact_gated_update_kernel(
                     start=True,
                     stop=True,
                 )
-                if i == len(OUT_CHUNKS) - 1 and c == 1:
+                if i == last - 1 or (i, c) in ((last - 2, 2), (last, 1)):
                     nc.vector.tensor_scalar_add(result[:, c, cols], bank[:], bo_cols[:, c : c + 1])
                 else:
                     nc.scalar.activation(
                         result[:, c, cols], bank[:], IDENT, bias=bo_cols[:, c : c + 1]
                     )
-                if i == len(OUT_CHUNKS) - 1:
-                    queue = nc.sync if c == 1 else nc.scalar
-                    queue.dma_start(out_view[:, c, cols], result[:, c, cols])
-            if i < len(OUT_CHUNKS) - 1:
+                if i in (last - 2, last):
+                    stored = slice(starts[i - 1] if i == last else starts[i], cols.stop)
+                    queue = nc.scalar if (i, c) == (last, 2) else nc.sync
+                    queue.dma_start(out_view[:, c, stored], result[:, c, stored])
+            if i < last - 2:
                 nc.sync.dma_start(out_view[:, :, cols], result[:, :, cols])
 
+        last = len(OUT_CHUNKS) - 1
         gate(SLOTS - 1, 0, HALF)
         gate(SLOTS - 1, HALF, HALF)
-        last = len(OUT_CHUNKS) - 1
-        for i in range(last + 2):
-            if i <= last:
-                make_h(i)
+        for i in range(last + 1):
+            make_h(i)
             if i > 0:
                 quantise_h(i - 1)
-                if i - 1 == WO_CHUNK:
-                    for earlier in range(WO_CHUNK):
-                        finish(earlier)
-                if i - 1 >= WO_CHUNK:
-                    finish(i - 1)
+            if 0 < i < last - 1:
+                finish(i - 1)
+        quantise_h(last)
+        for i in range(last - 2, last + 1):
+            finish(i)

@@ -21,8 +21,7 @@ PASSES = K // 512
 SLOTS = 4
 HALF = 512
 OUT_TILES = N // P
-OUT_CHUNKS = [128, 256, 128, 256, 128, 128]
-WO_CHUNK = 0
+OUT_CHUNKS = [256, 256, 256, 128, 128]
 
 
 def tile_list_contact_gated_update_kernel(
@@ -34,25 +33,29 @@ def tile_list_contact_gated_update_kernel(
         psum = ctx.enter_context(tc.psum_pool(name="psum", bufs=4))
         psum_b = ctx.enter_context(tc.psum_pool(name="psum_b", bufs=4))
 
-        def sb(name, shape, dtype, tag=None):
-            return keep.tile(shape, dtype, name=name, tag=tag or name, align_bytes=64)
+        shared = ctx.enter_context(tc.tile_pool(name="shared", bufs=1))
+
+        def sb(name, shape, dtype, at=None):
+            if at is None:
+                return keep.tile(shape, dtype, name=name, tag=name, align_bytes=64)
+            return shared.tile(shape, dtype, name=name, tag=name, align_bytes=64, offset=at)
 
         offsets = keep.tile([P, S // 16], U16, name="offsets")
 
         def picks(first, count):
             return offsets[:, first // 16 : (first + count) // 16]
 
-        scale_win = sb("scale_win", [P, T // 4], I32)
+        scale_win = sb("scale_win", [P, T // 4], I32, at=5120)
         wbs_raw = sb("wbs_raw", [P, PASSES, H // 4], I32)
         ba_cols = sb("ba_cols", [P, SLOTS], F32)
         bo_cols = sb("bo_cols", [P, OUT_TILES], F32)
         v_scales = sb("v_scales", [P, S // 4], I32)
         v_scales_low = sb("v_scales_low", [P, PASSES - 1, S // 4], I32)
-        nc.gpsimd.memset(scale_win[:], 0)
-        nc.vector.memset(wbs_raw[:], 0)
+        nc.gpsimd.memset(wbs_raw[:], 0)
+        nc.vector.memset(scale_win[:], 0)
         nc.vector.memset(v_scales_low[:], 0)
 
-        wa_raw = [sb(f"wa_raw{a}", [P, SLOTS, H], F32) for a in range(PASSES)]
+        wa_raw = [sb(f"wa_raw{a}", [P, SLOTS, H], F32, at=16384 if a == 1 else None) for a in range(PASSES)]
         tab = [sb(f"tab{a}", [P, T], I32) for a in range(PASSES)]
         wbw_raw = sb("wbw_raw", [P, PASSES, H // 2], I32)
         gates = [sb(f"gates{t}", [P, T], F32) for t in range(SLOTS)]
@@ -82,44 +85,33 @@ def tile_list_contact_gated_update_kernel(
         def lower_plane(a):
             nc.sync.dma_start(v_scales_low[0:112, a - 1, :], v_scales[4 * a : 4 * a + 112, :])
 
-        nc.sync.dma_start(wbw_raw[:], wb_words.bitcast(I32).rearrange("a p c -> p a c"))
-        load_wa(0)
         nc.sync.dma_start(offsets[:], offs)
-        for quad in range(4):
-            load_tab_scales(quad)
-        load_tab(0)
-        load_wa(1)
-        load_wa(2)
-        load_tab(1)
-        load_tab(2)
+        nc.sync.dma_start(wbw_raw[:], wb_words.bitcast(I32).rearrange("a p c -> p a c"))
         for row in range(4):
             load_wb_scales(row)
-
-        nc.vector.tensor_copy(
-            v_scales[:].bitcast(U8), scale_win[:].bitcast(U8).indirect(offsets[:])
-        )
-        nc.sync.dma_start(ba_cols[:], ba.rearrange("(p t) -> p t", t=SLOTS))
-        lower_plane(2)
-        lower_plane(1)
-        nc.sync.dma_start(gates[0][:], g_view[0])
-        for t in range(1, SLOTS):
-            nc.sync.dma_start(gates[t][:], g_view[t])
-        nc.sync.dma_start(wo_raw[:], wo.rearrange("(p t) n -> p t n", t=SLOTS))
-        with nc.allow_non_contiguous_dma(reason="one bias value for each partition"):
-            nc.sync.dma_start(bo_cols[:], bo.rearrange("(c p) -> p c", p=P))
+        load_tab(0)
+        load_tab(1)
+        for quad in range(4):
+            load_tab_scales(quad)
+        load_tab(2)
+        load_wa(0)
+        load_wa(1)
 
         wa_bf = [sb(f"wa_bf{a}", [P, SLOTS, P * 4], BF16) for a in range(PASSES)]
         wa_codes = [sb(f"wa_codes{a}", [P, H], U32) for a in range(PASSES)]
         wa_scales = [sb(f"wa_scales{a}", [P, H], U8) for a in range(PASSES)]
         v_words = {
-            (a, half): sb(f"v_words{a}{half}", [P, HALF], U32) for a in range(PASSES) for half in range(2)
+            (a, half): sb(f"v_words{a}{half}", [P, HALF], U32, at=None if a == 0 else 4096 * (a - 1) + 2048 * half)
+            for a in range(PASSES)
+            for half in range(2)
         }
+        wb_codes = sb("wb_codes", [P, PASSES, H // 2], I32)
+        wb_planes = sb("wb_planes", [P, PASSES, H // 4], I32)
 
-        def round_wa(a):
+        def round_wa(a, engines):
             src = wa_raw[a][:].rearrange("p j (m t) -> p m j t", t=SLOTS)
             dst = wa_bf[a][:].rearrange("p t (m j) -> p m j t", j=4)
-            for t in range(0, SLOTS, 2):
-                copy = nc.vector.tensor_copy if a > 0 and t == 0 else nc.scalar.copy
+            for t, copy in zip(range(0, SLOTS, 2), engines):
                 copy(dst[:, :, :, t : t + 2], src[:, :, :, t : t + 2])
 
         def quantise_wa(a):
@@ -135,126 +127,122 @@ def tile_list_contact_gated_update_kernel(
                     v_words[a, half][:], tab[a][:].bitcast(U32).indirect(picks(half * HALF, HALF))
                 )
 
-        a_banks = {}
-        for t in range(SLOTS):
-            for half in range(2):
-                a_banks[t, half] = psum.tile([P, HALF], F32, name="bank")
-
-        def a_pass(a, t, half):
-            cols = slice(half * HALF, (half + 1) * HALF)
-            nc.tensor.matmul_mx(
-                out=a_banks[t, half][:],
-                lhsT=wa_codes[a][:, t * P : (t + 1) * P].bitcast(FP8X4),
-                lhsT_scale=wa_scales[a][:, t * P : (t + 1) * P],
-                rhs=v_words[a, half][:].bitcast(FP8X4),
-                rhs_scale=v_scales[4 * a : P, :].bitcast(U8)[:, cols],
-                start=(a == 0),
-                stop=(a == PASSES - 1),
-            )
-
-        wb_codes = sb("wb_codes", [P, PASSES, H // 2], I32)
-        wb_planes = sb("wb_planes", [P, PASSES, H // 4], I32)
-
-        def reorder_wb_codes():
-            nc.vector.tensor_copy(
-                wb_codes[:].bitcast(U16).rearrange("p a (t m) -> p t a m", t=SLOTS),
-                wbw_raw[:].bitcast(U16).rearrange("p a (m t) -> p t a m", t=SLOTS),
-            )
-
-        def reorder_wb_planes():
-            nc.vector.tensor_copy(
-                wb_planes[:].bitcast(U8).rearrange("p a (t m) -> p t a m", t=SLOTS),
-                wbs_raw[:].bitcast(U8).rearrange("p a (m t) -> p t a m", t=SLOTS),
-            )
-
-        reorder_wb_codes()
-        for a in range(PASSES):
-            round_wa(a)
-            quantise_wa(a)
-            if a == 0:
-                gather_words(0)
+        nc.vector.tensor_copy(
+            wb_codes[:].bitcast(U16).rearrange("p a (t m) -> p t a m", t=SLOTS),
+            wbw_raw[:].bitcast(U16).rearrange("p a (m t) -> p t a m", t=SLOTS),
+        )
+        nc.vector.tensor_copy(
+            wb_planes[:].bitcast(U8).rearrange("p a (t m) -> p t a m", t=SLOTS),
+            wbs_raw[:].bitcast(U8).rearrange("p a (m t) -> p t a m", t=SLOTS),
+        )
+        gather_words(0)
         gather_words(1)
-        gather_words(2)
-        reorder_wb_planes()
+        nc.vector.tensor_copy(
+            v_scales[:].bitcast(U8), scale_win[:].bitcast(U8).indirect(offsets[:])
+        )
+        load_wa(2)
+        lower_plane(1)
+        lower_plane(2)
+        nc.sync.dma_start(ba_cols[:], ba.rearrange("(p t) -> p t", t=SLOTS))
+        for t in range(SLOTS):
+            nc.sync.dma_start(gates[t][:], g_view[t])
+        nc.sync.dma_start(wo_raw[:], wo.rearrange("(p t) n -> p t n", t=SLOTS))
+        with nc.allow_non_contiguous_dma(reason="one bias value for each partition"):
+            nc.sync.dma_start(bo_cols[:], bo.rearrange("(c p) -> p c", p=P))
 
+        gather_words(2)
+        on_vector, on_scalar = nc.vector.tensor_copy, nc.scalar.copy
+        round_wa(0, (on_scalar, on_scalar))
+        quantise_wa(0)
+        round_wa(1, (on_scalar, on_scalar))
+        quantise_wa(1)
+        round_wa(2, (on_vector, on_vector))
+        quantise_wa(2)
+
+        b_sums = sb("b_sums", [P, SLOTS, S], F32, at=16384)
         a_biased = sb("a_biased", [P, SLOTS, S], F32)
         gated = sb("gated", [P, SLOTS, S], F32)
+
+        def make_b(t, half):
+            cols = slice(half * HALF, (half + 1) * HALF)
+            bank = psum_b.tile([P, HALF], F32, name="bank")
+            for a in range(PASSES):
+                plane = v_scales[:] if a == 0 else v_scales_low[:, a - 1, :]
+                nc.tensor.matmul_mx(
+                    out=bank[:],
+                    lhsT=wb_codes[:, a, 64 * t : 64 * (t + 1)].bitcast(U8).bitcast(FP4X4),
+                    lhsT_scale=wb_planes[:, a, 32 * t : 32 * (t + 1)].bitcast(U8),
+                    rhs=v_words[a, half][:].bitcast(FP8X4),
+                    rhs_scale=plane.bitcast(U8)[:, cols],
+                    start=(a == 0),
+                    stop=(a == PASSES - 1),
+                )
+            nc.scalar.copy(b_sums[:, t, cols], bank[:])
+
+        def make_a(t, half):
+            cols = slice(half * HALF, (half + 1) * HALF)
+            bank = psum.tile([P, HALF], F32, name="bank")
+            for a in range(PASSES):
+                nc.tensor.matmul_mx(
+                    out=bank[:],
+                    lhsT=wa_codes[a][:, t * P : (t + 1) * P].bitcast(FP8X4),
+                    lhsT_scale=wa_scales[a][:, t * P : (t + 1) * P],
+                    rhs=v_words[a, half][:].bitcast(FP8X4),
+                    rhs_scale=v_scales[4 * a : P, :].bitcast(U8)[:, cols],
+                    start=(a == 0),
+                    stop=(a == PASSES - 1),
+                )
+            nc.scalar.activation(a_biased[:, t, cols], bank[:], IDENT, bias=ba_cols[:, t : t + 1])
 
         def gate(t, first, count):
             cols = slice(first, first + count)
             nc.vector.tensor_tensor(
-                gated[:, t, cols], gates[t][:].indirect(picks(first, count)), a_biased[:, t, cols], MULT
+                gated[:, t, cols], gates[t][:].indirect(picks(first, count)), b_sums[:, t, cols], MULT
             )
 
         for t in range(SLOTS):
             for half in range(2):
-                for a in range(PASSES):
-                    a_pass(a, t, half)
-                nc.scalar.activation(
-                    a_biased[:, t, half * HALF : (half + 1) * HALF],
-                    a_banks[t, half][:],
-                    IDENT,
-                    bias=ba_cols[:, t : t + 1],
-                )
-            if t == 0:
-                gate(t, 0, HALF)
-                gate(t, HALF, HALF)
-            elif t < SLOTS - 1:
+                make_b(t, half)
+            if t < SLOTS - 1:
                 gate(t, 0, S)
-
-        def b_group(target, t, cols):
-            for a in reversed(range(PASSES)):
-                plane = v_scales[:] if a == 0 else v_scales_low[:, a - 1, :]
-                nc.tensor.matmul_mx(
-                    out=target,
-                    lhsT=wb_codes[:, a, 64 * t : 64 * (t + 1)].bitcast(U8).bitcast(FP4X4),
-                    lhsT_scale=wb_planes[:, a, 32 * t : 32 * (t + 1)].bitcast(U8),
-                    rhs=v_words[a, cols.start // HALF][:, cols.start % HALF : (cols.stop - 1) % HALF + 1].bitcast(FP8X4),
-                    rhs_scale=plane.bitcast(U8)[:, cols],
-                    start=(a == PASSES - 1),
-                    stop=(a == 0),
-                )
-
-        b_sums = sb("b_sums", [P, SLOTS, HALF], F32)
-        for t in range(SLOTS):
-            bank = psum_b.tile([P, HALF], F32, name="bank")
-            b_group(bank[:], t, slice(0, HALF))
-            nc.scalar.copy(b_sums[:, t, :], bank[:])
-        b_blocks = {}
-        for first in range(HALF, S, P):
-            b_blocks[first] = psum_b.tile([P, SLOTS, P], F32, name="bank")
+        for half in range(2):
             for t in range(SLOTS):
-                b_group(b_blocks[first][:, t, :], t, slice(first, first + P))
+                make_a(t, half)
+
+        wo_bf = sb("wo_bf", [P, N, SLOTS], BF16, at=8704)
+        wo_codes = sb("wo_codes", [P, N], U32)
+        wo_scales = sb("wo_scales", [P, N], U8)
+        nc.scalar.copy(
+            wo_bf[:].rearrange("p (n i) t -> p n t i", i=4),
+            wo_raw[:].rearrange("p t (n i) -> p n t i", i=4),
+        )
+
+        def quantise_wo():
+            for cols in (slice(0, 2 * P), slice(2 * P, N)):
+                nc.vector.quantize_mx(
+                    out=wo_codes[:, cols].bitcast(FP8X4),
+                    scales=wo_scales[:, cols],
+                    in_=wo_bf[:, cols, :].rearrange("p n t -> p (n t)"),
+                )
 
         result = sb("result", [P, OUT_TILES, S], F32)
         out_view = out.rearrange("(c p) j -> p c j", p=P)
         starts = [sum(OUT_CHUNKS[:i]) for i in range(len(OUT_CHUNKS))]
+        last = len(OUT_CHUNKS) - 1
         h_bf, codes, scales = {}, {}, {}
 
         def make_h(i):
-            lead = N if i == WO_CHUNK else 0
-            width = lead + OUT_CHUNKS[i]
-            h_bf[i] = sb(f"h_bf{i}", [P, width, SLOTS], BF16, tag="h_bf0" if i == 2 else None)
+            width = OUT_CHUNKS[i]
+            cols = slice(starts[i], starts[i] + width)
+            h_bf[i] = sb(f"h_bf{i}", [P, width, SLOTS], BF16, at=None if i == 0 else 8192 + 2048 * ((i - 1) % 2))
             codes[i] = sb(f"codes{i}", [P, width], U32)
             scales[i] = sb(f"scales{i}", [P, width], U8)
-            if i == WO_CHUNK:
-                nc.scalar.copy(
-                    h_bf[i][:, 0:N, :].rearrange("p (n i) t -> p n t i", i=4),
-                    wo_raw[:].rearrange("p t (n i) -> p n t i", i=4),
-                )
-            start, end = starts[i], starts[i] + OUT_CHUNKS[i]
-            pieces = [(start, min(end, HALF))] if start < HALF else []
-            pieces.extend((first, min(first + P, end)) for first in range(max(start, HALF), end, P))
-            for first, last in pieces:
-                block = first - first % P
-                b_part = b_sums[:, :, first:last] if first < HALF else b_blocks[block][:, :, first - block : last - block]
-                shift = lead - start
-                nc.vector.tensor_tensor(
-                    h_bf[i][:, first + shift : last + shift, :].rearrange("p (n i) t -> p n t i", i=4),
-                    b_part.rearrange("p t (n i) -> p n t i", i=4),
-                    gated[:, :, first:last].rearrange("p t (n i) -> p n t i", i=4),
-                    MULT,
-                )
+            nc.vector.tensor_tensor(
+                h_bf[i][:].rearrange("p (n i) t -> p n t i", i=4),
+                a_biased[:, :, cols].rearrange("p t (n i) -> p n t i", i=4),
+                gated[:, :, cols].rearrange("p t (n i) -> p n t i", i=4),
+                MULT,
+            )
 
         def quantise_h(i):
             nc.vector.quantize_mx(
@@ -264,43 +252,35 @@ def tile_list_contact_gated_update_kernel(
             )
 
         def finish(i):
-            lead = N if i == WO_CHUNK else 0
             count = OUT_CHUNKS[i]
             cols = slice(starts[i], starts[i] + count)
             for c in range(OUT_TILES):
-                pool = psum_b if i == last - 1 or (i == last and c == 0) else psum
+                pool = psum_b if (OUT_TILES * i + c) % 2 == 0 else psum
                 bank = pool.tile([P, count], F32, name="bank")
                 nc.tensor.matmul_mx(
                     out=bank[:],
-                    lhsT=codes[WO_CHUNK][:, c * P : (c + 1) * P].bitcast(FP8X4),
-                    lhsT_scale=scales[WO_CHUNK][:, c * P : (c + 1) * P],
-                    rhs=codes[i][:, lead : lead + count].bitcast(FP8X4),
-                    rhs_scale=scales[i][:, lead : lead + count],
+                    lhsT=wo_codes[:, c * P : (c + 1) * P].bitcast(FP8X4),
+                    lhsT_scale=wo_scales[:, c * P : (c + 1) * P],
+                    rhs=codes[i][:].bitcast(FP8X4),
+                    rhs_scale=scales[i][:],
                     start=True,
                     stop=True,
                 )
-                if i == last - 1 or (i, c) in ((last - 2, 2), (last, 1)):
+                if (i, c) == (last, 1):
                     nc.vector.tensor_scalar_add(result[:, c, cols], bank[:], bo_cols[:, c : c + 1])
                 else:
                     nc.scalar.activation(
                         result[:, c, cols], bank[:], IDENT, bias=bo_cols[:, c : c + 1]
                     )
-                if i in (last - 2, last):
-                    stored = slice(starts[i - 1] if i == last else starts[i], cols.stop)
-                    queue = nc.scalar if (i, c) == (last, 2) else nc.sync
-                    queue.dma_start(out_view[:, c, stored], result[:, c, stored])
-            if i < last - 2:
-                nc.sync.dma_start(out_view[:, :, cols], result[:, :, cols])
+            nc.sync.dma_start(out_view[:, :, cols], result[:, :, cols])
 
-        last = len(OUT_CHUNKS) - 1
+        quantise_wo()
         gate(SLOTS - 1, 0, HALF)
+        make_h(0)
         gate(SLOTS - 1, HALF, HALF)
-        for i in range(last + 1):
+        for i in range(1, last + 1):
             make_h(i)
-            if i > 0:
-                quantise_h(i - 1)
-            if 0 < i < last - 1:
-                finish(i - 1)
+            quantise_h(i - 1)
+            finish(i - 1)
         quantise_h(last)
-        for i in range(last - 2, last + 1):
-            finish(i)
+        finish(last)

@@ -30,8 +30,7 @@ def tile_list_contact_gated_update_kernel(
     nc = tc.nc
     with ExitStack() as ctx:
         keep = ctx.enter_context(tc.tile_pool(name="keep", bufs=1))
-        psum = ctx.enter_context(tc.psum_pool(name="psum", bufs=4))
-        psum_b = ctx.enter_context(tc.psum_pool(name="psum_b", bufs=4))
+        psum = ctx.enter_context(tc.psum_pool(name="psum", bufs=8))
 
         shared = ctx.enter_context(tc.tile_pool(name="shared", bufs=1))
 
@@ -45,7 +44,7 @@ def tile_list_contact_gated_update_kernel(
         def picks(first, count):
             return offsets[:, first // 16 : (first + count) // 16]
 
-        scale_win = sb("scale_win", [P, T // 4], I32, at=5120)
+        scale_win = sb("scale_win", [P, T // 4], I32, at=1024)
         wbs_raw = sb("wbs_raw", [P, PASSES, H // 4], I32)
         ba_cols = sb("ba_cols", [P, SLOTS], F32)
         bo_cols = sb("bo_cols", [P, OUT_TILES], F32)
@@ -136,13 +135,12 @@ def tile_list_contact_gated_update_kernel(
             wbs_raw[:].bitcast(U8).rearrange("p a (m t) -> p t a m", t=SLOTS),
         )
         gather_words(0)
-        gather_words(1)
         nc.vector.tensor_copy(
             v_scales[:].bitcast(U8), scale_win[:].bitcast(U8).indirect(offsets[:])
         )
-        load_wa(2)
         lower_plane(1)
         lower_plane(2)
+        load_wa(2)
         nc.sync.dma_start(ba_cols[:], ba.rearrange("(p t) -> p t", t=SLOTS))
         for t in range(SLOTS):
             nc.sync.dma_start(gates[t][:], g_view[t])
@@ -150,6 +148,7 @@ def tile_list_contact_gated_update_kernel(
         with nc.allow_non_contiguous_dma(reason="one bias value for each partition"):
             nc.sync.dma_start(bo_cols[:], bo.rearrange("(c p) -> p c", p=P))
 
+        gather_words(1)
         gather_words(2)
         on_vector, on_scalar = nc.vector.tensor_copy, nc.scalar.copy
         round_wa(0, (on_scalar, on_scalar))
@@ -165,7 +164,7 @@ def tile_list_contact_gated_update_kernel(
 
         def make_b(t, half):
             cols = slice(half * HALF, (half + 1) * HALF)
-            bank = psum_b.tile([P, HALF], F32, name="bank")
+            bank = psum.tile([P, HALF], F32, name="bank")
             for a in range(PASSES):
                 plane = v_scales[:] if a == 0 else v_scales_low[:, a - 1, :]
                 nc.tensor.matmul_mx(
@@ -255,8 +254,7 @@ def tile_list_contact_gated_update_kernel(
             count = OUT_CHUNKS[i]
             cols = slice(starts[i], starts[i] + count)
             for c in range(OUT_TILES):
-                pool = psum_b if (OUT_TILES * i + c) % 2 == 0 else psum
-                bank = pool.tile([P, count], F32, name="bank")
+                bank = psum.tile([P, count], F32, name="bank")
                 nc.tensor.matmul_mx(
                     out=bank[:],
                     lhsT=wo_codes[:, c * P : (c + 1) * P].bitcast(FP8X4),
@@ -272,7 +270,11 @@ def tile_list_contact_gated_update_kernel(
                     nc.scalar.activation(
                         result[:, c, cols], bank[:], IDENT, bias=bo_cols[:, c : c + 1]
                     )
-            nc.sync.dma_start(out_view[:, :, cols], result[:, :, cols])
+                if i == last:
+                    queue = nc.scalar if c == OUT_TILES - 1 else nc.sync
+                    queue.dma_start(out_view[:, c, cols], result[:, c, cols])
+            if i < last:
+                nc.sync.dma_start(out_view[:, :, cols], result[:, :, cols])
 
         quantise_wo()
         gate(SLOTS - 1, 0, HALF)

@@ -21,7 +21,7 @@ PASSES = K // 512
 SLOTS = 4
 HALF = 512
 OUT_TILES = N // P
-OUT_CHUNKS = [256, 256, 256, 128, 128]
+OUT_CHUNKS = [512, 128, 128, 128, 128]
 
 
 def tile_list_contact_gated_update_kernel(
@@ -50,7 +50,7 @@ def tile_list_contact_gated_update_kernel(
         bo_cols = sb("bo_cols", [P, OUT_TILES], F32)
         v_scales = sb("v_scales", [P, S // 4], I32)
         v_scales_low = sb("v_scales_low", [P, PASSES - 1, S // 4], I32)
-        nc.gpsimd.memset(wbs_raw[:], 0)
+        nc.vector.memset(wbs_raw[:], 0)
         nc.vector.memset(scale_win[:], 0)
         nc.vector.memset(v_scales_low[:], 0)
 
@@ -58,7 +58,7 @@ def tile_list_contact_gated_update_kernel(
         tab = [sb(f"tab{a}", [P, T], I32) for a in range(PASSES)]
         wbw_raw = sb("wbw_raw", [P, PASSES, H // 2], I32)
         gates = [sb(f"gates{t}", [P, T], F32) for t in range(SLOTS)]
-        wo_raw = sb("wo_raw", [P, SLOTS, N], F32)
+        wo_raw = sb("wo_raw", [P, SLOTS, N], F32, at=8192)
         g_view = gT.rearrange("(p t) c -> t p c", t=SLOTS)
 
         def load_wa(a):
@@ -176,7 +176,7 @@ def tile_list_contact_gated_update_kernel(
                     start=(a == 0),
                     stop=(a == PASSES - 1),
                 )
-            nc.scalar.copy(b_sums[:, t, cols], bank[:])
+            return bank
 
         def make_a(t, half):
             cols = slice(half * HALF, (half + 1) * HALF)
@@ -193,31 +193,39 @@ def tile_list_contact_gated_update_kernel(
                 )
             nc.scalar.activation(a_biased[:, t, cols], bank[:], IDENT, bias=ba_cols[:, t : t + 1])
 
-        def gate(t, first, count):
+        def gate(t, first, count, b_part=None):
             cols = slice(first, first + count)
+            b_part = b_sums[:, t, cols] if b_part is None else b_part
             nc.vector.tensor_tensor(
-                gated[:, t, cols], gates[t][:].indirect(picks(first, count)), b_sums[:, t, cols], MULT
+                gated[:, t, cols], gates[t][:].indirect(picks(first, count)), b_part, MULT
             )
 
         for t in range(SLOTS):
             for half in range(2):
-                make_b(t, half)
+                b_bank = make_b(t, half)
+                if (t, half) != (SLOTS - 1, 1):
+                    nc.scalar.copy(b_sums[:, t, half * HALF : (half + 1) * HALF], b_bank[:])
             if t < SLOTS - 1:
                 gate(t, 0, S)
         for half in range(2):
             for t in range(SLOTS):
                 make_a(t, half)
 
-        wo_bf = sb("wo_bf", [P, N, SLOTS], BF16, at=8704)
+        wo_bf = sb("wo_bf", [P, N, SLOTS], BF16)
         wo_codes = sb("wo_codes", [P, N], U32)
         wo_scales = sb("wo_scales", [P, N], U8)
-        nc.scalar.copy(
-            wo_bf[:].rearrange("p (n i) t -> p n t i", i=4),
-            wo_raw[:].rearrange("p t (n i) -> p n t i", i=4),
-        )
+        wo_parts = [slice(c * P, (c + 1) * P) for c in range(OUT_TILES)]
+        for cols in wo_parts:
+            nc.scalar.copy(
+                wo_bf[:, cols, :].rearrange("p (n i) t -> p n t i", i=4),
+                wo_raw[:, :, cols].rearrange("p t (n i) -> p n t i", i=4),
+            )
+
+        b_last = sb("b_last", [P, HALF], F32, at=8192)
+        nc.scalar.copy(b_last[:], b_bank[:])
 
         def quantise_wo():
-            for cols in (slice(0, 2 * P), slice(2 * P, N)):
+            for cols in wo_parts:
                 nc.vector.quantize_mx(
                     out=wo_codes[:, cols].bitcast(FP8X4),
                     scales=wo_scales[:, cols],
@@ -233,15 +241,18 @@ def tile_list_contact_gated_update_kernel(
         def make_h(i):
             width = OUT_CHUNKS[i]
             cols = slice(starts[i], starts[i] + width)
-            h_bf[i] = sb(f"h_bf{i}", [P, width, SLOTS], BF16, at=None if i == 0 else 8192 + 2048 * ((i - 1) % 2))
+            h_bf[i] = sb(f"h_bf{i}", [P, width, SLOTS], BF16)
             codes[i] = sb(f"codes{i}", [P, width], U32)
             scales[i] = sb(f"scales{i}", [P, width], U8)
-            nc.vector.tensor_tensor(
-                h_bf[i][:].rearrange("p (n i) t -> p n t i", i=4),
-                a_biased[:, :, cols].rearrange("p t (n i) -> p n t i", i=4),
-                gated[:, :, cols].rearrange("p t (n i) -> p n t i", i=4),
-                MULT,
-            )
+            for first in range(0, width, HALF // 2):
+                count = min(width, HALF // 2)
+                part = slice(cols.start + first, cols.start + first + count)
+                nc.vector.tensor_tensor(
+                    h_bf[i][:, first : first + count, :].rearrange("p (n i) t -> p n t i", i=4),
+                    a_biased[:, :, part].rearrange("p t (n i) -> p n t i", i=4),
+                    gated[:, :, part].rearrange("p t (n i) -> p n t i", i=4),
+                    MULT,
+                )
 
         def quantise_h(i):
             nc.vector.quantize_mx(
@@ -264,23 +275,29 @@ def tile_list_contact_gated_update_kernel(
                     start=True,
                     stop=True,
                 )
-                if (i, c) == (last, 1):
+                if (i, c) in ((last - 1, 2), (last, 1)):
                     nc.vector.tensor_scalar_add(result[:, c, cols], bank[:], bo_cols[:, c : c + 1])
                 else:
                     nc.scalar.activation(
                         result[:, c, cols], bank[:], IDENT, bias=bo_cols[:, c : c + 1]
                     )
-                if i == last:
-                    queue = nc.scalar if c == OUT_TILES - 1 else nc.sync
+                if i in (0, last):
+                    queue = nc.scalar if (i, c) == (last, OUT_TILES - 1) else nc.sync
                     queue.dma_start(out_view[:, c, cols], result[:, c, cols])
-            if i < last:
+            if 0 < i < last:
                 nc.sync.dma_start(out_view[:, :, cols], result[:, :, cols])
 
-        quantise_wo()
-        gate(SLOTS - 1, 0, HALF)
+        piece = HALF // 2
+        gate(SLOTS - 1, 0, piece)
+        gate(SLOTS - 1, piece, piece)
         make_h(0)
-        gate(SLOTS - 1, HALF, HALF)
-        for i in range(1, last + 1):
+        quantise_wo()
+        quantise_h(0)
+        finish(0)
+        gate(SLOTS - 1, 2 * piece, piece, b_last[:, 0:piece])
+        gate(SLOTS - 1, 3 * piece, piece, b_last[:, piece:HALF])
+        make_h(1)
+        for i in range(2, last + 1):
             make_h(i)
             quantise_h(i - 1)
             finish(i - 1)

@@ -44,7 +44,7 @@ def tile_list_contact_gated_update_kernel(
         def picks(first, count):
             return offsets[:, first // 16 : (first + count) // 16]
 
-        scale_win = sb("scale_win", [P, T // 4], I32, at=1024)
+        scale_win = sb("scale_win", [P, T // 4], I32, at=3072)
         wbs_raw = sb("wbs_raw", [P, PASSES, H // 4], I32)
         ba_cols = sb("ba_cols", [P, SLOTS], F32)
         bo_cols = sb("bo_cols", [P, OUT_TILES], F32)
@@ -69,11 +69,11 @@ def tile_list_contact_gated_update_kernel(
         def load_tab(a):
             nc.sync.dma_start(tab[a][:], tab_words[a].rearrange("p t i -> p (t i)").bitcast(I32))
 
-        def load_tab_scales(quad):
-            nc.sync.dma_start(
-                scale_win[32 * quad : 32 * quad + 4 * PASSES, :],
-                tab_scales[:, 4 * quad : 4 * quad + 4, :].bitcast(I32),
-            )
+        def load_first_scales(row):
+            nc.sync.dma_start(scale_win[row:P:32, :], tab_scales[0, row:16:4, :].bitcast(I32))
+
+        def load_spread_scales(a):
+            nc.sync.dma_start(scale_win[3 + a : P : 8, :], tab_scales[a].bitcast(I32))
 
         def load_wb_scales(row):
             nc.sync.dma_start(
@@ -81,8 +81,12 @@ def tile_list_contact_gated_update_kernel(
                 wb_scales[:, row:16:4, :].bitcast(I32).rearrange("a q c -> q a c"),
             )
 
-        def lower_plane(a):
-            nc.sync.dma_start(v_scales_low[0:112, a - 1, :], v_scales[4 * a : 4 * a + 112, :])
+        def move_scales(first, count):
+            for move in range(first, first + count):
+                a, row = 1 + move // 4, move % 4
+                nc.sync.dma_start(
+                    v_scales_low[row:P:32, a - 1, :], v_scales[8 * row + 3 + a : P : 32, :]
+                )
 
         nc.sync.dma_start(offsets[:], offs)
         nc.sync.dma_start(wbw_raw[:], wb_words.bitcast(I32).rearrange("a p c -> p a c"))
@@ -90,20 +94,19 @@ def tile_list_contact_gated_update_kernel(
             load_wb_scales(row)
         load_tab(0)
         load_tab(1)
-        for quad in range(4):
-            load_tab_scales(quad)
+        load_spread_scales(1)
+        load_spread_scales(2)
+        for row in range(4):
+            load_first_scales(row)
         load_tab(2)
         load_wa(0)
-        load_wa(1)
 
         wa_bf = [sb(f"wa_bf{a}", [P, SLOTS, P * 4], BF16) for a in range(PASSES)]
         wa_codes = [sb(f"wa_codes{a}", [P, H], U32) for a in range(PASSES)]
         wa_scales = [sb(f"wa_scales{a}", [P, H], U8) for a in range(PASSES)]
-        v_words = {
-            (a, half): sb(f"v_words{a}{half}", [P, HALF], U32, at=None if a == 0 else 4096 * (a - 1) + 2048 * half)
-            for a in range(PASSES)
-            for half in range(2)
-        }
+        v_words = [
+            sb(f"v_words{a}", [P, S], U32, at=None if a == 0 else 4096 * (a - 1)) for a in range(PASSES)
+        ]
         wb_codes = sb("wb_codes", [P, PASSES, H // 2], I32)
         wb_planes = sb("wb_planes", [P, PASSES, H // 4], I32)
 
@@ -121,10 +124,7 @@ def tile_list_contact_gated_update_kernel(
             )
 
         def gather_words(a):
-            for half in range(2):
-                nc.vector.tensor_copy(
-                    v_words[a, half][:], tab[a][:].bitcast(U32).indirect(picks(half * HALF, HALF))
-                )
+            nc.vector.tensor_copy(v_words[a][:], tab[a][:].bitcast(U32).indirect(offsets[:]))
 
         nc.vector.tensor_copy(
             wb_codes[:].bitcast(U16).rearrange("p a (t m) -> p t a m", t=SLOTS),
@@ -138,8 +138,9 @@ def tile_list_contact_gated_update_kernel(
         nc.vector.tensor_copy(
             v_scales[:].bitcast(U8), scale_win[:].bitcast(U8).indirect(offsets[:])
         )
-        lower_plane(1)
-        lower_plane(2)
+        move_scales(0, 2)
+        load_wa(1)
+        move_scales(2, 6)
         load_wa(2)
         nc.sync.dma_start(ba_cols[:], ba.rearrange("(p t) -> p t", t=SLOTS))
         for t in range(SLOTS):
@@ -162,17 +163,20 @@ def tile_list_contact_gated_update_kernel(
         a_biased = sb("a_biased", [P, SLOTS, S], F32)
         gated = sb("gated", [P, SLOTS, S], F32)
 
+        def v_plane(a, cols):
+            plane = v_scales[:] if a == 0 else v_scales_low[:, a - 1, :]
+            return plane.bitcast(U8)[:, cols]
+
         def make_b(t, half):
             cols = slice(half * HALF, (half + 1) * HALF)
             bank = psum.tile([P, HALF], F32, name="bank")
             for a in range(PASSES):
-                plane = v_scales[:] if a == 0 else v_scales_low[:, a - 1, :]
                 nc.tensor.matmul_mx(
                     out=bank[:],
                     lhsT=wb_codes[:, a, 64 * t : 64 * (t + 1)].bitcast(U8).bitcast(FP4X4),
                     lhsT_scale=wb_planes[:, a, 32 * t : 32 * (t + 1)].bitcast(U8),
-                    rhs=v_words[a, half][:].bitcast(FP8X4),
-                    rhs_scale=plane.bitcast(U8)[:, cols],
+                    rhs=v_words[a][:, cols].bitcast(FP8X4),
+                    rhs_scale=v_plane(a, cols),
                     start=(a == 0),
                     stop=(a == PASSES - 1),
                 )
@@ -186,8 +190,8 @@ def tile_list_contact_gated_update_kernel(
                     out=bank[:],
                     lhsT=wa_codes[a][:, t * P : (t + 1) * P].bitcast(FP8X4),
                     lhsT_scale=wa_scales[a][:, t * P : (t + 1) * P],
-                    rhs=v_words[a, half][:].bitcast(FP8X4),
-                    rhs_scale=v_scales[4 * a : P, :].bitcast(U8)[:, cols],
+                    rhs=v_words[a][:, cols].bitcast(FP8X4),
+                    rhs_scale=v_plane(a, cols),
                     start=(a == 0),
                     stop=(a == PASSES - 1),
                 )

@@ -20,8 +20,16 @@ P = 128
 PASSES = K // 512
 SLOTS = 4
 HALF = 512
+PIECE = HALF // 2
 OUT_TILES = N // P
-OUT_CHUNKS = [512, 128, 128, 128, 128]
+OUT_CHUNKS = [HALF, 128, 128, 128, 128]
+SPARE_ROW = 3
+EARLY_MOVES = 2
+
+WORDS_AT = (0, 4096)
+SCALE_WINDOW_AT = 3072
+WO_RAW_AT = 8192
+WA1_RAW_AT = 16384
 
 
 def tile_list_contact_gated_update_kernel(
@@ -31,7 +39,6 @@ def tile_list_contact_gated_update_kernel(
     with ExitStack() as ctx:
         keep = ctx.enter_context(tc.tile_pool(name="keep", bufs=1))
         psum = ctx.enter_context(tc.psum_pool(name="psum", bufs=8))
-
         shared = ctx.enter_context(tc.tile_pool(name="shared", bufs=1))
 
         def sb(name, shape, dtype, at=None):
@@ -44,103 +51,105 @@ def tile_list_contact_gated_update_kernel(
         def picks(first, count):
             return offsets[:, first // 16 : (first + count) // 16]
 
-        scale_win = sb("scale_win", [P, T // 4], I32, at=3072)
+        scale_win = sb("scale_win", [P, T // 4], I32, at=SCALE_WINDOW_AT)
         wbs_raw = sb("wbs_raw", [P, PASSES, H // 4], I32)
         ba_cols = sb("ba_cols", [P, SLOTS], F32)
         bo_cols = sb("bo_cols", [P, OUT_TILES], F32)
         v_scales = sb("v_scales", [P, S // 4], I32)
-        v_scales_low = sb("v_scales_low", [P, PASSES - 1, S // 4], I32)
+        v_scales_moved = sb("v_scales_moved", [P, PASSES - 1, S // 4], I32)
         nc.vector.memset(wbs_raw[:], 0)
         nc.vector.memset(scale_win[:], 0)
-        nc.vector.memset(v_scales_low[:], 0)
+        nc.vector.memset(v_scales_moved[:], 0)
 
-        wa_raw = [sb(f"wa_raw{a}", [P, SLOTS, H], F32, at=16384 if a == 1 else None) for a in range(PASSES)]
-        tab = [sb(f"tab{a}", [P, T], I32) for a in range(PASSES)]
+        wa_raw = [
+            sb(f"wa_raw{s}", [P, 4, H], F32, at=WA1_RAW_AT if s == 1 else None) for s in range(PASSES)
+        ]
+        tab = [sb(f"tab{s}", [P, T], I32) for s in range(PASSES)]
         wbw_raw = sb("wbw_raw", [P, PASSES, H // 2], I32)
         gates = [sb(f"gates{t}", [P, T], F32) for t in range(SLOTS)]
-        wo_raw = sb("wo_raw", [P, SLOTS, N], F32, at=8192)
+        wo_raw = sb("wo_raw", [P, SLOTS, N], F32, at=WO_RAW_AT)
         g_view = gT.rearrange("(p t) c -> t p c", t=SLOTS)
 
-        def load_wa(a):
+        def load_wa(s):
             nc.sync.dma_start(
-                wa_raw[a][:], wa[512 * a : 512 * (a + 1), :].rearrange("(p j) c -> p j c", j=4)
+                wa_raw[s][:], wa[512 * s : 512 * (s + 1), :].rearrange("(p j) c -> p j c", j=4)
             )
 
-        def load_tab(a):
-            nc.sync.dma_start(tab[a][:], tab_words[a].rearrange("p t i -> p (t i)").bitcast(I32))
-
-        def load_first_scales(row):
-            nc.sync.dma_start(scale_win[row:P:32, :], tab_scales[0, row:16:4, :].bitcast(I32))
-
-        def load_spread_scales(a):
-            nc.sync.dma_start(scale_win[3 + a : P : 8, :], tab_scales[a].bitcast(I32))
+        def load_tab(s):
+            nc.sync.dma_start(tab[s][:], tab_words[s].rearrange("p t i -> p (t i)").bitcast(I32))
 
         def load_wb_scales(row):
             nc.sync.dma_start(
                 wbs_raw[row:P:32, :, :],
-                wb_scales[:, row:16:4, :].bitcast(I32).rearrange("a q c -> q a c"),
+                wb_scales[:, row:16:4, :].bitcast(I32).rearrange("s q c -> q s c"),
             )
 
-        def move_scales(first, count):
-            for move in range(first, first + count):
-                a, row = 1 + move // 4, move % 4
+        def load_first_scales(row):
+            nc.sync.dma_start(scale_win[row:P:32, :], tab_scales[0, row:16:4, :].bitcast(I32))
+
+        def load_spread_scales(s):
+            nc.sync.dma_start(scale_win[SPARE_ROW + s : P : 8, :], tab_scales[s].bitcast(I32))
+
+        def move_scales(moves):
+            for move in moves:
+                s, row = 1 + move // 4, move % 4
                 nc.sync.dma_start(
-                    v_scales_low[row:P:32, a - 1, :], v_scales[8 * row + 3 + a : P : 32, :]
+                    v_scales_moved[row:P:32, s - 1, :], v_scales[8 * row + SPARE_ROW + s : P : 32, :]
                 )
 
         nc.sync.dma_start(offsets[:], offs)
-        nc.sync.dma_start(wbw_raw[:], wb_words.bitcast(I32).rearrange("a p c -> p a c"))
+        nc.sync.dma_start(wbw_raw[:], wb_words.bitcast(I32).rearrange("s p c -> p s c"))
         for row in range(4):
             load_wb_scales(row)
         load_tab(0)
-        load_tab(1)
-        load_spread_scales(1)
-        load_spread_scales(2)
+        for s in range(1, PASSES):
+            load_spread_scales(s)
         for row in range(4):
             load_first_scales(row)
+        load_tab(1)
         load_tab(2)
         load_wa(0)
 
-        wa_bf = [sb(f"wa_bf{a}", [P, SLOTS, P * 4], BF16) for a in range(PASSES)]
-        wa_codes = [sb(f"wa_codes{a}", [P, H], U32) for a in range(PASSES)]
-        wa_scales = [sb(f"wa_scales{a}", [P, H], U8) for a in range(PASSES)]
+        wa_bf = [sb(f"wa_bf{s}", [P, SLOTS, P * 4], BF16) for s in range(PASSES)]
+        wa_codes = [sb(f"wa_codes{s}", [P, H], U32) for s in range(PASSES)]
+        wa_scales = [sb(f"wa_scales{s}", [P, H], U8) for s in range(PASSES)]
         v_words = [
-            sb(f"v_words{a}", [P, S], U32, at=None if a == 0 else 4096 * (a - 1)) for a in range(PASSES)
+            sb(f"v_words{s}", [P, S], U32, at=WORDS_AT[s] if s < len(WORDS_AT) else None) for s in range(PASSES)
         ]
         wb_codes = sb("wb_codes", [P, PASSES, H // 2], I32)
         wb_planes = sb("wb_planes", [P, PASSES, H // 4], I32)
 
-        def round_wa(a, engines):
-            src = wa_raw[a][:].rearrange("p j (m t) -> p m j t", t=SLOTS)
-            dst = wa_bf[a][:].rearrange("p t (m j) -> p m j t", j=4)
-            for t, copy in zip(range(0, SLOTS, 2), engines):
+        def round_wa(s, copies):
+            src = wa_raw[s][:].rearrange("p j (m t) -> p m j t", t=SLOTS)
+            dst = wa_bf[s][:].rearrange("p t (m j) -> p m j t", j=4)
+            for t, copy in zip(range(0, SLOTS, 2), copies):
                 copy(dst[:, :, :, t : t + 2], src[:, :, :, t : t + 2])
 
-        def quantise_wa(a):
+        def quantise_wa(s):
             nc.vector.quantize_mx(
-                out=wa_codes[a][:].bitcast(FP8X4),
-                scales=wa_scales[a][:],
-                in_=wa_bf[a][:].rearrange("p t c -> p (t c)"),
+                out=wa_codes[s][:].bitcast(FP8X4),
+                scales=wa_scales[s][:],
+                in_=wa_bf[s][:].rearrange("p t c -> p (t c)"),
             )
 
-        def gather_words(a):
-            nc.vector.tensor_copy(v_words[a][:], tab[a][:].bitcast(U32).indirect(offsets[:]))
+        def gather_words(s):
+            nc.vector.tensor_copy(v_words[s][:], tab[s][:].bitcast(U32).indirect(offsets[:]))
 
         nc.vector.tensor_copy(
-            wb_codes[:].bitcast(U16).rearrange("p a (t m) -> p t a m", t=SLOTS),
-            wbw_raw[:].bitcast(U16).rearrange("p a (m t) -> p t a m", t=SLOTS),
+            wb_codes[:].bitcast(U16).rearrange("p s (t m) -> p t s m", t=SLOTS),
+            wbw_raw[:].bitcast(U16).rearrange("p s (m t) -> p t s m", t=SLOTS),
         )
         nc.vector.tensor_copy(
-            wb_planes[:].bitcast(U8).rearrange("p a (t m) -> p t a m", t=SLOTS),
-            wbs_raw[:].bitcast(U8).rearrange("p a (m t) -> p t a m", t=SLOTS),
+            wb_planes[:].bitcast(U8).rearrange("p s (t m) -> p t s m", t=SLOTS),
+            wbs_raw[:].bitcast(U8).rearrange("p s (m t) -> p t s m", t=SLOTS),
         )
-        gather_words(0)
         nc.vector.tensor_copy(
             v_scales[:].bitcast(U8), scale_win[:].bitcast(U8).indirect(offsets[:])
         )
-        move_scales(0, 2)
+        gather_words(0)
+        move_scales(range(EARLY_MOVES))
         load_wa(1)
-        move_scales(2, 6)
+        move_scales(range(EARLY_MOVES, 4 * (PASSES - 1)))
         load_wa(2)
         nc.sync.dma_start(ba_cols[:], ba.rearrange("(p t) -> p t", t=SLOTS))
         for t in range(SLOTS):
@@ -151,106 +160,102 @@ def tile_list_contact_gated_update_kernel(
 
         gather_words(1)
         gather_words(2)
-        on_vector, on_scalar = nc.vector.tensor_copy, nc.scalar.copy
+        on_scalar, on_vector = nc.scalar.copy, nc.vector.tensor_copy
         round_wa(0, (on_scalar, on_scalar))
+        round_wa(1, (on_scalar, on_vector))
         quantise_wa(0)
-        round_wa(1, (on_scalar, on_scalar))
         quantise_wa(1)
         round_wa(2, (on_vector, on_vector))
         quantise_wa(2)
 
-        b_sums = sb("b_sums", [P, SLOTS, S], F32, at=16384)
+        b_sums = sb("b_sums", [P, SLOTS, S], F32, at=WA1_RAW_AT)
         a_biased = sb("a_biased", [P, SLOTS, S], F32)
         gated = sb("gated", [P, SLOTS, S], F32)
 
-        def v_plane(a, cols):
-            plane = v_scales[:] if a == 0 else v_scales_low[:, a - 1, :]
+        def v_plane(s, cols):
+            plane = v_scales[:] if s == 0 else v_scales_moved[:, s - 1, :]
             return plane.bitcast(U8)[:, cols]
 
-        def make_b(t, half):
-            cols = slice(half * HALF, (half + 1) * HALF)
+        def make_b(t, cols):
             bank = psum.tile([P, HALF], F32, name="bank")
-            for a in range(PASSES):
+            for s in range(PASSES):
                 nc.tensor.matmul_mx(
                     out=bank[:],
-                    lhsT=wb_codes[:, a, 64 * t : 64 * (t + 1)].bitcast(U8).bitcast(FP4X4),
-                    lhsT_scale=wb_planes[:, a, 32 * t : 32 * (t + 1)].bitcast(U8),
-                    rhs=v_words[a][:, cols].bitcast(FP8X4),
-                    rhs_scale=v_plane(a, cols),
-                    start=(a == 0),
-                    stop=(a == PASSES - 1),
+                    lhsT=wb_codes[:, s, 64 * t : 64 * (t + 1)].bitcast(U8).bitcast(FP4X4),
+                    lhsT_scale=wb_planes[:, s, 32 * t : 32 * (t + 1)].bitcast(U8),
+                    rhs=v_words[s][:, cols].bitcast(FP8X4),
+                    rhs_scale=v_plane(s, cols),
+                    start=(s == 0),
+                    stop=(s == PASSES - 1),
                 )
             return bank
 
-        def make_a(t, half):
-            cols = slice(half * HALF, (half + 1) * HALF)
+        def make_a(t, cols):
             bank = psum.tile([P, HALF], F32, name="bank")
-            for a in range(PASSES):
+            for s in range(PASSES):
                 nc.tensor.matmul_mx(
                     out=bank[:],
-                    lhsT=wa_codes[a][:, t * P : (t + 1) * P].bitcast(FP8X4),
-                    lhsT_scale=wa_scales[a][:, t * P : (t + 1) * P],
-                    rhs=v_words[a][:, cols].bitcast(FP8X4),
-                    rhs_scale=v_plane(a, cols),
-                    start=(a == 0),
-                    stop=(a == PASSES - 1),
+                    lhsT=wa_codes[s][:, t * P : (t + 1) * P].bitcast(FP8X4),
+                    lhsT_scale=wa_scales[s][:, t * P : (t + 1) * P],
+                    rhs=v_words[s][:, cols].bitcast(FP8X4),
+                    rhs_scale=v_plane(s, cols),
+                    start=(s == 0),
+                    stop=(s == PASSES - 1),
                 )
             nc.scalar.activation(a_biased[:, t, cols], bank[:], IDENT, bias=ba_cols[:, t : t + 1])
 
-        def gate(t, first, count, b_part=None):
-            cols = slice(first, first + count)
-            b_part = b_sums[:, t, cols] if b_part is None else b_part
+        def gate(t, first, count, b_part):
             nc.vector.tensor_tensor(
-                gated[:, t, cols], gates[t][:].indirect(picks(first, count)), b_part, MULT
+                gated[:, t, first : first + count], gates[t][:].indirect(picks(first, count)), b_part, MULT
             )
 
-        for t in range(SLOTS):
-            for half in range(2):
-                b_bank = make_b(t, half)
-                if (t, half) != (SLOTS - 1, 1):
-                    nc.scalar.copy(b_sums[:, t, half * HALF : (half + 1) * HALF], b_bank[:])
-            if t < SLOTS - 1:
-                gate(t, 0, S)
-        for half in range(2):
+        halves = [slice(0, HALF), slice(HALF, S)]
+        last_slot = SLOTS - 1
+        for t in range(last_slot):
+            for cols in halves:
+                nc.scalar.copy(b_sums[:, t, cols], make_b(t, cols)[:])
+            gate(t, 0, S, b_sums[:, t, :])
+        nc.scalar.copy(b_sums[:, last_slot, halves[0]], make_b(last_slot, halves[0])[:])
+        b_last_bank = make_b(last_slot, halves[1])
+        for cols in halves:
             for t in range(SLOTS):
-                make_a(t, half)
+                make_a(t, cols)
 
         wo_bf = sb("wo_bf", [P, N, SLOTS], BF16)
         wo_codes = sb("wo_codes", [P, N], U32)
         wo_scales = sb("wo_scales", [P, N], U8)
-        wo_parts = [slice(c * P, (c + 1) * P) for c in range(OUT_TILES)]
-        for cols in wo_parts:
+        out_rows = [slice(c * P, (c + 1) * P) for c in range(OUT_TILES)]
+        for rows in out_rows:
             nc.scalar.copy(
-                wo_bf[:, cols, :].rearrange("p (n i) t -> p n t i", i=4),
-                wo_raw[:, :, cols].rearrange("p t (n i) -> p n t i", i=4),
+                wo_bf[:, rows, :].rearrange("p (n i) t -> p n t i", i=4),
+                wo_raw[:, :, rows].rearrange("p t (n i) -> p n t i", i=4),
             )
 
-        b_last = sb("b_last", [P, HALF], F32, at=8192)
-        nc.scalar.copy(b_last[:], b_bank[:])
+        b_last = sb("b_last", [P, HALF], F32, at=WO_RAW_AT)
+        nc.scalar.copy(b_last[:], b_last_bank[:])
 
         def quantise_wo():
-            for cols in wo_parts:
+            for rows in out_rows:
                 nc.vector.quantize_mx(
-                    out=wo_codes[:, cols].bitcast(FP8X4),
-                    scales=wo_scales[:, cols],
-                    in_=wo_bf[:, cols, :].rearrange("p n t -> p (n t)"),
+                    out=wo_codes[:, rows].bitcast(FP8X4),
+                    scales=wo_scales[:, rows],
+                    in_=wo_bf[:, rows, :].rearrange("p n t -> p (n t)"),
                 )
 
         result = sb("result", [P, OUT_TILES, S], F32)
         out_view = out.rearrange("(c p) j -> p c j", p=P)
         starts = [sum(OUT_CHUNKS[:i]) for i in range(len(OUT_CHUNKS))]
         last = len(OUT_CHUNKS) - 1
-        h_bf, codes, scales = {}, {}, {}
+        h_bf, h_codes, h_scales = {}, {}, {}
 
         def make_h(i):
             width = OUT_CHUNKS[i]
-            cols = slice(starts[i], starts[i] + width)
             h_bf[i] = sb(f"h_bf{i}", [P, width, SLOTS], BF16)
-            codes[i] = sb(f"codes{i}", [P, width], U32)
-            scales[i] = sb(f"scales{i}", [P, width], U8)
-            for first in range(0, width, HALF // 2):
-                count = min(width, HALF // 2)
-                part = slice(cols.start + first, cols.start + first + count)
+            h_codes[i] = sb(f"h_codes{i}", [P, width], U32)
+            h_scales[i] = sb(f"h_scales{i}", [P, width], U8)
+            count = min(width, PIECE)
+            for first in range(0, width, count):
+                part = slice(starts[i] + first, starts[i] + first + count)
                 nc.vector.tensor_tensor(
                     h_bf[i][:, first : first + count, :].rearrange("p (n i) t -> p n t i", i=4),
                     a_biased[:, :, part].rearrange("p t (n i) -> p n t i", i=4),
@@ -260,22 +265,23 @@ def tile_list_contact_gated_update_kernel(
 
         def quantise_h(i):
             nc.vector.quantize_mx(
-                out=codes[i][:].bitcast(FP8X4),
-                scales=scales[i][:],
+                out=h_codes[i][:].bitcast(FP8X4),
+                scales=h_scales[i][:],
                 in_=h_bf[i][:].rearrange("p n t -> p (n t)"),
             )
 
         def finish(i):
             count = OUT_CHUNKS[i]
             cols = slice(starts[i], starts[i] + count)
-            for c in range(OUT_TILES):
+            by_tile = i in (0, last - 1, last)
+            for c, rows in enumerate(out_rows):
                 bank = psum.tile([P, count], F32, name="bank")
                 nc.tensor.matmul_mx(
                     out=bank[:],
-                    lhsT=wo_codes[:, c * P : (c + 1) * P].bitcast(FP8X4),
-                    lhsT_scale=wo_scales[:, c * P : (c + 1) * P],
-                    rhs=codes[i][:].bitcast(FP8X4),
-                    rhs_scale=scales[i][:],
+                    lhsT=wo_codes[:, rows].bitcast(FP8X4),
+                    lhsT_scale=wo_scales[:, rows],
+                    rhs=h_codes[i][:].bitcast(FP8X4),
+                    rhs_scale=h_scales[i][:],
                     start=True,
                     stop=True,
                 )
@@ -285,21 +291,20 @@ def tile_list_contact_gated_update_kernel(
                     nc.scalar.activation(
                         result[:, c, cols], bank[:], IDENT, bias=bo_cols[:, c : c + 1]
                     )
-                if i in (0, last):
+                if by_tile:
                     queue = nc.scalar if (i, c) == (last, OUT_TILES - 1) else nc.sync
                     queue.dma_start(out_view[:, c, cols], result[:, c, cols])
-            if 0 < i < last:
+            if not by_tile:
                 nc.sync.dma_start(out_view[:, :, cols], result[:, :, cols])
 
-        piece = HALF // 2
-        gate(SLOTS - 1, 0, piece)
-        gate(SLOTS - 1, piece, piece)
+        for first in range(0, HALF, PIECE):
+            gate(last_slot, first, PIECE, b_sums[:, last_slot, first : first + PIECE])
         make_h(0)
         quantise_wo()
         quantise_h(0)
         finish(0)
-        gate(SLOTS - 1, 2 * piece, piece, b_last[:, 0:piece])
-        gate(SLOTS - 1, 3 * piece, piece, b_last[:, piece:HALF])
+        for first in range(0, HALF, PIECE):
+            gate(last_slot, HALF + first, PIECE, b_last[:, first : first + PIECE])
         make_h(1)
         for i in range(2, last + 1):
             make_h(i)

@@ -257,9 +257,9 @@ def tile_list_contact_gated_update_kernel(
             for first in range(0, width, count):
                 part = slice(starts[i] + first, starts[i] + first + count)
                 nc.vector.tensor_tensor(
-                    h_bf[i][:, first : first + count, :].rearrange("p (n i) t -> p n t i", i=4),
-                    a_biased[:, :, part].rearrange("p t (n i) -> p n t i", i=4),
-                    gated[:, :, part].rearrange("p t (n i) -> p n t i", i=4),
+                    h_bf[i][:, first : first + count, :].rearrange("p (n i) t -> p n t i", i=2),
+                    a_biased[:, :, part].rearrange("p t (n i) -> p n t i", i=2),
+                    gated[:, :, part].rearrange("p t (n i) -> p n t i", i=2),
                     MULT,
                 )
 

@@ -23,13 +23,19 @@ HALF = 512
 PIECE = HALF // 2
 OUT_TILES = N // P
 OUT_CHUNKS = [HALF, 128, 128, 128, 128]
-SPARE_ROW = 3
-EARLY_MOVES = 2
+V_PLANE = S // 4
+WB_PLANE = H // 4
+MOVES_IN_A_RUN = 6
 
-WORDS_AT = (0, 4096)
-SCALE_WINDOW_AT = 3072
-WO_RAW_AT = 8192
-WA1_RAW_AT = 16384
+BIG = 8192
+TAB_AT = (BIG + BIG // 2, 5 * BIG + BIG // 2 + 64, 3 * BIG)
+WA_RAW_AT = (4 * BIG + 64, BIG, 2 * BIG)
+B_SUMS_AT = 0
+BA_AT = WA_RAW_AT[0] - 64
+V_SCALES_AT = BA_AT
+GATES_AT = (TAB_AT[1] - BIG // 2, TAB_AT[2], TAB_AT[1] + BIG // 2, WA_RAW_AT[0])
+WO_RAW_AT = WA_RAW_AT[2]
+BO_AT = WO_RAW_AT + SLOTS * N * 4
 
 
 def tile_list_contact_gated_update_kernel(
@@ -51,22 +57,22 @@ def tile_list_contact_gated_update_kernel(
         def picks(first, count):
             return offsets[:, first // 16 : (first + count) // 16]
 
-        scale_win = sb("scale_win", [P, T // 4], I32, at=SCALE_WINDOW_AT)
-        wbs_raw = sb("wbs_raw", [P, PASSES, H // 4], I32)
-        ba_cols = sb("ba_cols", [P, SLOTS], F32)
-        bo_cols = sb("bo_cols", [P, OUT_TILES], F32)
-        v_scales = sb("v_scales", [P, S // 4], I32)
-        v_scales_moved = sb("v_scales_moved", [P, PASSES - 1, S // 4], I32)
-        nc.vector.memset(wbs_raw[:], 0)
+        scale_win = sb("scale_win", [P, T // 4], I32)
+        wbs_raw = sb("wbs_raw", [P, WB_PLANE], I32)
+        ba_cols = sb("ba_cols", [P, SLOTS], F32, at=BA_AT)
+        bo_cols = sb("bo_cols", [P, OUT_TILES], F32, at=BO_AT)
+        v_scales = sb("v_scales", [P, V_PLANE], I32, at=V_SCALES_AT)
+        spread = sb("spread", [P, V_PLANE + WB_PLANE], I32)
+        planes = [sb(f"planes{s}", [P, V_PLANE + WB_PLANE], I32) for s in range(PASSES)]
         nc.vector.memset(scale_win[:], 0)
-        nc.vector.memset(v_scales_moved[:], 0)
+        nc.gpsimd.memset(wbs_raw[:], 0)
+        for plane in planes:
+            nc.vector.memset(plane[:], 0)
 
-        wa_raw = [
-            sb(f"wa_raw{s}", [P, 4, H], F32, at=WA1_RAW_AT if s == 1 else None) for s in range(PASSES)
-        ]
-        tab = [sb(f"tab{s}", [P, T], I32) for s in range(PASSES)]
+        wa_raw = [sb(f"wa_raw{s}", [P, 4, H], F32, at=WA_RAW_AT[s]) for s in range(PASSES)]
+        tab = [sb(f"tab{s}", [P, T], I32, at=TAB_AT[s]) for s in range(PASSES)]
         wbw_raw = sb("wbw_raw", [P, PASSES, H // 2], I32)
-        gates = [sb(f"gates{t}", [P, T], F32) for t in range(SLOTS)]
+        gates = [sb(f"gates{t}", [P, T], F32, at=GATES_AT[t]) for t in range(SLOTS)]
         wo_raw = sb("wo_raw", [P, SLOTS, N], F32, at=WO_RAW_AT)
         g_view = gT.rearrange("(p t) c -> t p c", t=SLOTS)
 
@@ -78,46 +84,32 @@ def tile_list_contact_gated_update_kernel(
         def load_tab(s):
             nc.sync.dma_start(tab[s][:], tab_words[s].rearrange("p t i -> p (t i)").bitcast(I32))
 
-        def load_wb_scales(row):
-            nc.sync.dma_start(
-                wbs_raw[row:P:32, :, :],
-                wb_scales[:, row:16:4, :].bitcast(I32).rearrange("s q c -> q s c"),
-            )
-
-        def load_first_scales(row):
-            nc.sync.dma_start(scale_win[row:P:32, :], tab_scales[0, row:16:4, :].bitcast(I32))
-
-        def load_spread_scales(s):
-            nc.sync.dma_start(scale_win[SPARE_ROW + s : P : 8, :], tab_scales[s].bitcast(I32))
+        def load_spread(tile, rows):
+            nc.sync.dma_start(tile[0:P:4, :], rows[0:2].rearrange("s q c -> (s q) c").bitcast(I32))
+            nc.sync.dma_start(tile[1:P:8, :], rows[2].bitcast(I32))
 
         def move_scales(moves):
             for move in moves:
-                s, row = 1 + move // 4, move % 4
-                nc.sync.dma_start(
-                    v_scales_moved[row:P:32, s - 1, :], v_scales[8 * row + SPARE_ROW + s : P : 32, :]
-                )
+                s, row = divmod(move, 4)
+                if s < 2:
+                    rows = slice(64 * s + 4 * row, 64 * (s + 1), 16)
+                else:
+                    rows = slice(8 * row + 1, P, 32)
+                nc.sync.dma_start(planes[s][row:P:32, :], spread[rows, :])
 
         nc.sync.dma_start(offsets[:], offs)
         nc.sync.dma_start(wbw_raw[:], wb_words.bitcast(I32).rearrange("s p c -> p s c"))
-        for row in range(4):
-            load_wb_scales(row)
-        load_tab(0)
-        for s in range(1, PASSES):
-            load_spread_scales(s)
-        for row in range(4):
-            load_first_scales(row)
-        load_tab(1)
-        load_tab(2)
-        load_wa(0)
+        load_spread(scale_win, tab_scales)
+        load_spread(wbs_raw, wb_scales)
+        for s in range(PASSES):
+            load_tab(s)
 
         wa_bf = [sb(f"wa_bf{s}", [P, SLOTS, P * 4], BF16) for s in range(PASSES)]
         wa_codes = [sb(f"wa_codes{s}", [P, H], U32) for s in range(PASSES)]
         wa_scales = [sb(f"wa_scales{s}", [P, H], U8) for s in range(PASSES)]
-        v_words = [
-            sb(f"v_words{s}", [P, S], U32, at=WORDS_AT[s] if s < len(WORDS_AT) else None) for s in range(PASSES)
-        ]
+        v_words = [sb(f"v_words{s}", [P, S], U32) for s in range(PASSES)]
         wb_codes = sb("wb_codes", [P, PASSES, H // 2], I32)
-        wb_planes = sb("wb_planes", [P, PASSES, H // 4], I32)
+
 
         def round_wa(s, copies):
             src = wa_raw[s][:].rearrange("p j (m t) -> p m j t", t=SLOTS)
@@ -140,41 +132,43 @@ def tile_list_contact_gated_update_kernel(
             wbw_raw[:].bitcast(U16).rearrange("p s (m t) -> p t s m", t=SLOTS),
         )
         nc.vector.tensor_copy(
-            wb_planes[:].bitcast(U8).rearrange("p s (t m) -> p t s m", t=SLOTS),
-            wbs_raw[:].bitcast(U8).rearrange("p s (m t) -> p t s m", t=SLOTS),
+            spread[:, V_PLANE:].bitcast(U8).rearrange("p (t m) -> p t m", t=SLOTS),
+            wbs_raw[:].bitcast(U8).rearrange("p (m t) -> p t m", t=SLOTS),
         )
         nc.vector.tensor_copy(
             v_scales[:].bitcast(U8), scale_win[:].bitcast(U8).indirect(offsets[:])
         )
+        nc.vector.tensor_copy(spread[:, :V_PLANE], v_scales[:])
+        move_scales(range(MOVES_IN_A_RUN))
+        load_wa(0)
+        move_scales(range(MOVES_IN_A_RUN, 4 * PASSES))
         gather_words(0)
-        move_scales(range(EARLY_MOVES))
         load_wa(1)
-        move_scales(range(EARLY_MOVES, 4 * (PASSES - 1)))
         load_wa(2)
         nc.sync.dma_start(ba_cols[:], ba.rearrange("(p t) -> p t", t=SLOTS))
-        for t in range(SLOTS):
-            nc.sync.dma_start(gates[t][:], g_view[t])
-        nc.sync.dma_start(wo_raw[:], wo.rearrange("(p t) n -> p t n", t=SLOTS))
-        with nc.allow_non_contiguous_dma(reason="one bias value for each partition"):
-            nc.sync.dma_start(bo_cols[:], bo.rearrange("(c p) -> p c", p=P))
-
         gather_words(1)
+        nc.sync.dma_start(gates[0][:], g_view[0])
         gather_words(2)
+        nc.sync.dma_start(gates[1][:], g_view[1])
+        nc.sync.dma_start(gates[2][:], g_view[2])
         on_scalar, on_vector = nc.scalar.copy, nc.vector.tensor_copy
         round_wa(0, (on_scalar, on_scalar))
+        nc.sync.dma_start(gates[3][:], g_view[3])
         round_wa(1, (on_scalar, on_vector))
         quantise_wa(0)
         quantise_wa(1)
         round_wa(2, (on_vector, on_vector))
         quantise_wa(2)
+        nc.sync.dma_start(wo_raw[:], wo.rearrange("(p t) n -> p t n", t=SLOTS))
+        with nc.allow_non_contiguous_dma(reason="one bias value for each partition"):
+            nc.sync.dma_start(bo_cols[:], bo.rearrange("(c p) -> p c", p=P))
 
-        b_sums = sb("b_sums", [P, SLOTS, S], F32, at=WA1_RAW_AT)
+        b_sums = sb("b_sums", [P, SLOTS, S], F32, at=B_SUMS_AT)
         a_biased = sb("a_biased", [P, SLOTS, S], F32)
         gated = sb("gated", [P, SLOTS, S], F32)
 
         def v_plane(s, cols):
-            plane = v_scales[:] if s == 0 else v_scales_moved[:, s - 1, :]
-            return plane.bitcast(U8)[:, cols]
+            return planes[s][:, :V_PLANE].bitcast(U8)[:, cols]
 
         def make_b(t, cols):
             bank = psum.tile([P, HALF], F32, name="bank")
@@ -182,7 +176,7 @@ def tile_list_contact_gated_update_kernel(
                 nc.tensor.matmul_mx(
                     out=bank[:],
                     lhsT=wb_codes[:, s, 64 * t : 64 * (t + 1)].bitcast(U8).bitcast(FP4X4),
-                    lhsT_scale=wb_planes[:, s, 32 * t : 32 * (t + 1)].bitcast(U8),
+                    lhsT_scale=planes[s][:, V_PLANE + 32 * t : V_PLANE + 32 * (t + 1)].bitcast(U8),
                     rhs=v_words[s][:, cols].bitcast(FP8X4),
                     rhs_scale=v_plane(s, cols),
                     start=(s == 0),
@@ -257,9 +251,9 @@ def tile_list_contact_gated_update_kernel(
             for first in range(0, width, count):
                 part = slice(starts[i] + first, starts[i] + first + count)
                 nc.vector.tensor_tensor(
-                    h_bf[i][:, first : first + count, :].rearrange("p (n i) t -> p n t i", i=2),
-                    a_biased[:, :, part].rearrange("p t (n i) -> p n t i", i=2),
-                    gated[:, :, part].rearrange("p t (n i) -> p n t i", i=2),
+                    h_bf[i][:, first : first + count, :].rearrange("p (n i) t -> p n t i", i=4),
+                    a_biased[:, :, part].rearrange("p t (n i) -> p n t i", i=4),
+                    gated[:, :, part].rearrange("p t (n i) -> p n t i", i=4),
                     MULT,
                 )
 

@@ -35,6 +35,7 @@ BA_AT = WA_RAW_AT[0] - 64
 V_SCALES_AT = BA_AT
 GATES_AT = (TAB_AT[1] - BIG // 2, TAB_AT[2], TAB_AT[1] + BIG // 2, WA_RAW_AT[0])
 WO_RAW_AT = WA_RAW_AT[2]
+B_LAST_AT = BIG + BIG // 2
 BO_AT = WO_RAW_AT + SLOTS * N * 4
 
 
@@ -163,7 +164,8 @@ def tile_list_contact_gated_update_kernel(
         with nc.allow_non_contiguous_dma(reason="one bias value for each partition"):
             nc.sync.dma_start(bo_cols[:], bo.rearrange("(c p) -> p c", p=P))
 
-        b_sums = sb("b_sums", [P, SLOTS, S], F32, at=B_SUMS_AT)
+        b_sums = sb("b_sums", [P, SLOTS - 1, S], F32, at=B_SUMS_AT)
+        b_last = [sb(f"b_last{half}", [P, HALF], F32, at=B_LAST_AT) for half in range(2)]
         a_biased = sb("a_biased", [P, SLOTS, S], F32)
         gated = sb("gated", [P, SLOTS, S], F32)
 
@@ -209,7 +211,7 @@ def tile_list_contact_gated_update_kernel(
             for cols in halves:
                 nc.scalar.copy(b_sums[:, t, cols], make_b(t, cols)[:])
             gate(t, 0, S, b_sums[:, t, :])
-        nc.scalar.copy(b_sums[:, last_slot, halves[0]], make_b(last_slot, halves[0])[:])
+        nc.scalar.copy(b_last[0][:], make_b(last_slot, halves[0])[:])
         b_last_bank = make_b(last_slot, halves[1])
         for cols in halves:
             for t in range(SLOTS):
@@ -219,22 +221,13 @@ def tile_list_contact_gated_update_kernel(
         wo_codes = sb("wo_codes", [P, N], U32)
         wo_scales = sb("wo_scales", [P, N], U8)
         out_rows = [slice(c * P, (c + 1) * P) for c in range(OUT_TILES)]
-        for rows in out_rows:
-            nc.scalar.copy(
-                wo_bf[:, rows, :].rearrange("p (n i) t -> p n t i", i=4),
-                wo_raw[:, :, rows].rearrange("p t (n i) -> p n t i", i=4),
+        def quantise_wo(c):
+            rows = out_rows[c]
+            nc.vector.quantize_mx(
+                out=wo_codes[:, rows].bitcast(FP8X4),
+                scales=wo_scales[:, rows],
+                in_=wo_bf[:, rows, :].rearrange("p n t -> p (n t)"),
             )
-
-        b_last = sb("b_last", [P, HALF], F32, at=WO_RAW_AT)
-        nc.scalar.copy(b_last[:], b_last_bank[:])
-
-        def quantise_wo():
-            for rows in out_rows:
-                nc.vector.quantize_mx(
-                    out=wo_codes[:, rows].bitcast(FP8X4),
-                    scales=wo_scales[:, rows],
-                    in_=wo_bf[:, rows, :].rearrange("p n t -> p (n t)"),
-                )
 
         result = sb("result", [P, OUT_TILES, S], F32)
         out_view = out.rearrange("(c p) j -> p c j", p=P)
@@ -292,13 +285,21 @@ def tile_list_contact_gated_update_kernel(
                 nc.sync.dma_start(out_view[:, :, cols], result[:, :, cols])
 
         for first in range(0, HALF, PIECE):
-            gate(last_slot, first, PIECE, b_sums[:, last_slot, first : first + PIECE])
+            gate(last_slot, first, PIECE, b_last[0][:, first : first + PIECE])
+        nc.scalar.copy(b_last[1][:], b_last_bank[:])
+        for rows in out_rows:
+            nc.scalar.copy(
+                wo_bf[:, rows, :].rearrange("p (n i) t -> p n t i", i=4),
+                wo_raw[:, :, rows].rearrange("p t (n i) -> p n t i", i=4),
+            )
         make_h(0)
-        quantise_wo()
         quantise_h(0)
+        quantise_wo(0)
+        for piece in range(2):
+            first = piece * PIECE
+            gate(last_slot, HALF + first, PIECE, b_last[1][:, first : first + PIECE])
+            quantise_wo(piece + 1)
         finish(0)
-        for first in range(0, HALF, PIECE):
-            gate(last_slot, HALF + first, PIECE, b_last[:, first : first + PIECE])
         make_h(1)
         for i in range(2, last + 1):
             make_h(i)

@@ -260,7 +260,8 @@ def tile_list_contact_gated_update_kernel(
         def finish(i):
             count = OUT_CHUNKS[i]
             cols = slice(starts[i], starts[i] + count)
-            by_tile = i in (0, last - 1, last)
+            by_tile = i in (0, last)
+            stored = slice(starts[last - 1], S) if i == last else cols
             for c, rows in enumerate(out_rows):
                 bank = psum.tile([P, count], F32, name="bank")
                 nc.tensor.matmul_mx(
@@ -280,8 +281,8 @@ def tile_list_contact_gated_update_kernel(
                     )
                 if by_tile:
                     queue = nc.scalar if (i, c) == (last, OUT_TILES - 1) else nc.sync
-                    queue.dma_start(out_view[:, c, cols], result[:, c, cols])
-            if not by_tile:
+                    queue.dma_start(out_view[:, c, stored], result[:, c, stored])
+            if not by_tile and i != last - 1:
                 nc.sync.dma_start(out_view[:, :, cols], result[:, :, cols])
 
         for first in range(0, HALF, PIECE):

from contextlib import ExitStack

import concourse.mybir as mybir

K, H, N, T, S = 1536, 512, 384, 2048, 1024
FLOPS = 2 * S * (2 * K * H + H * N)

F32 = mybir.dt.float32
BF16 = mybir.dt.bfloat16
I32 = mybir.dt.int32
U32 = mybir.dt.uint32
U16 = mybir.dt.uint16
U8 = mybir.dt.uint8
FP8X4 = mybir.dt.float8_e4m3fn_x4
FP4X4 = mybir.dt.float4_e2m1fn_x4
MULT = mybir.AluOpType.mult
IDENT = mybir.ActivationFunctionType.Identity

P = 128
PASSES = K // 512
SLOTS = 4
HALF = 512
PIECE = HALF // 2
OUT_TILES = N // P
OUT_CHUNKS = [HALF, 128, 128, 128, 128]
V_PLANE = S // 4
WB_PLANE = H // 4
MOVES_IN_A_RUN = 6

BIG = 8192
TAB_AT = (BIG + BIG // 2, 5 * BIG + BIG // 2 + 64, 3 * BIG)
WA_RAW_AT = (4 * BIG + 64, BIG, 2 * BIG)
B_SUMS_AT = 0
BA_AT = WA_RAW_AT[0] - 64
V_SCALES_AT = BA_AT
GATES_AT = (TAB_AT[1] - BIG // 2, TAB_AT[2], TAB_AT[1] + BIG // 2, WA_RAW_AT[0])
WO_RAW_AT = WA_RAW_AT[2]
B_LAST_AT = BIG + BIG // 2
BO_AT = WO_RAW_AT + SLOTS * N * 4


def tile_list_contact_gated_update_kernel(
    tc, tab_words, tab_scales, offs, wa, ba, wb_words, wb_scales, gT, wo, bo, out
):
    nc = tc.nc
    with ExitStack() as ctx:
        keep = ctx.enter_context(tc.tile_pool(name="keep", bufs=1))
        psum = ctx.enter_context(tc.psum_pool(name="psum", bufs=8))
        shared = ctx.enter_context(tc.tile_pool(name="shared", bufs=1))

        def sb(name, shape, dtype, at=None):
            if at is None:
                return keep.tile(shape, dtype, name=name, tag=name, align_bytes=64)
            return shared.tile(shape, dtype, name=name, tag=name, align_bytes=64, offset=at)

        offsets = keep.tile([P, S // 16], U16, name="offsets")

        def picks(first, count):
            return offsets[:, first // 16 : (first + count) // 16]

        scale_win = sb("scale_win", [P, T // 4], I32)
        wbs_raw = sb("wbs_raw", [P, WB_PLANE], I32)
        ba_cols = sb("ba_cols", [P, SLOTS], F32, at=BA_AT)
        bo_cols = sb("bo_cols", [P, OUT_TILES], F32, at=BO_AT)
        v_scales = sb("v_scales", [P, V_PLANE], I32, at=V_SCALES_AT)
        spread = sb("spread", [P, V_PLANE + WB_PLANE], I32)
        planes = [sb(f"planes{s}", [P, V_PLANE + WB_PLANE], I32) for s in range(PASSES)]
        nc.vector.memset(scale_win[:], 0)
        nc.gpsimd.memset(wbs_raw[:], 0)
        for plane in planes:
            nc.vector.memset(plane[:], 0)

        wa_raw = [sb(f"wa_raw{s}", [P, 4, H], F32, at=WA_RAW_AT[s]) for s in range(PASSES)]
        tab = [sb(f"tab{s}", [P, T], I32, at=TAB_AT[s]) for s in range(PASSES)]
        wbw_raw = sb("wbw_raw", [P, PASSES, H // 2], I32)
        gates = [sb(f"gates{t}", [P, T], F32, at=GATES_AT[t]) for t in range(SLOTS)]
        wo_raw = sb("wo_raw", [P, SLOTS, N], F32, at=WO_RAW_AT)
        g_view = gT.rearrange("(p t) c -> t p c", t=SLOTS)

        def load_wa(s):
            nc.sync.dma_start(
                wa_raw[s][:], wa[512 * s : 512 * (s + 1), :].rearrange("(p j) c -> p j c", j=4)
            )

        def load_tab(s):
            nc.sync.dma_start(tab[s][:], tab_words[s].rearrange("p t i -> p (t i)").bitcast(I32))

        def load_spread(tile, rows):
            nc.sync.dma_start(tile[0:P:4, :], rows[0:2].rearrange("s q c -> (s q) c").bitcast(I32))
            nc.sync.dma_start(tile[1:P:8, :], rows[2].bitcast(I32))

        def move_scales(moves):
            for move in moves:
                s, row = divmod(move, 4)
                if s < 2:
                    rows = slice(64 * s + 4 * row, 64 * (s + 1), 16)
                else:
                    rows = slice(8 * row + 1, P, 32)
                nc.sync.dma_start(planes[s][row:P:32, :], spread[rows, :])

        nc.sync.dma_start(offsets[:], offs)
        nc.sync.dma_start(wbw_raw[:], wb_words.bitcast(I32).rearrange("s p c -> p s c"))
        load_spread(scale_win, tab_scales)
        load_spread(wbs_raw, wb_scales)
        for s in range(PASSES):
            load_tab(s)

        wa_bf = [sb(f"wa_bf{s}", [P, SLOTS, P * 4], BF16) for s in range(PASSES)]
        wa_codes = [sb(f"wa_codes{s}", [P, H], U32) for s in range(PASSES)]
        wa_scales = [sb(f"wa_scales{s}", [P, H], U8) for s in range(PASSES)]
        v_words = [sb(f"v_words{s}", [P, S], U32) for s in range(PASSES)]
        wb_codes = sb("wb_codes", [P, PASSES, H // 2], I32)


        def round_wa(s, copies):
            src = wa_raw[s][:].rearrange("p j (m t) -> p m j t", t=SLOTS)
            dst = wa_bf[s][:].rearrange("p t (m j) -> p m j t", j=4)
            for t, copy in zip(range(0, SLOTS, 2), copies):
                copy(dst[:, :, :, t : t + 2], src[:, :, :, t : t + 2])

        def quantise_wa(s):
            nc.vector.quantize_mx(
                out=wa_codes[s][:].bitcast(FP8X4),
                scales=wa_scales[s][:],
                in_=wa_bf[s][:].rearrange("p t c -> p (t c)"),
            )

        def gather_words(s):
            nc.vector.tensor_copy(v_words[s][:], tab[s][:].bitcast(U32).indirect(offsets[:]))

        nc.vector.tensor_copy(
            wb_codes[:].bitcast(U16).rearrange("p s (t m) -> p t s m", t=SLOTS),
            wbw_raw[:].bitcast(U16).rearrange("p s (m t) -> p t s m", t=SLOTS),
        )
        nc.vector.tensor_copy(
            spread[:, V_PLANE:].bitcast(U8).rearrange("p (t m) -> p t m", t=SLOTS),
            wbs_raw[:].bitcast(U8).rearrange("p (m t) -> p t m", t=SLOTS),
        )
        nc.vector.tensor_copy(
            v_scales[:].bitcast(U8), scale_win[:].bitcast(U8).indirect(offsets[:])
        )
        nc.vector.tensor_copy(spread[:, :V_PLANE], v_scales[:])
        move_scales(range(MOVES_IN_A_RUN))
        load_wa(0)
        move_scales(range(MOVES_IN_A_RUN, 4 * PASSES))
        gather_words(0)
        load_wa(1)
        load_wa(2)
        nc.sync.dma_start(ba_cols[:], ba.rearrange("(p t) -> p t", t=SLOTS))
        gather_words(1)
        nc.sync.dma_start(gates[0][:], g_view[0])
        gather_words(2)
        nc.sync.dma_start(gates[1][:], g_view[1])
        nc.sync.dma_start(gates[2][:], g_view[2])
        on_scalar, on_vector = nc.scalar.copy, nc.vector.tensor_copy
        round_wa(0, (on_scalar, on_scalar))
        nc.sync.dma_start(gates[3][:], g_view[3])
        round_wa(1, (on_scalar, on_vector))
        quantise_wa(0)
        quantise_wa(1)
        round_wa(2, (on_vector, on_vector))
        quantise_wa(2)
        nc.sync.dma_start(wo_raw[:], wo.rearrange("(p t) n -> p t n", t=SLOTS))
        with nc.allow_non_contiguous_dma(reason="one bias value for each partition"):
            nc.sync.dma_start(bo_cols[:], bo.rearrange("(c p) -> p c", p=P))

        b_sums = sb("b_sums", [P, SLOTS - 1, S], F32, at=B_SUMS_AT)
        b_last = [sb(f"b_last{half}", [P, HALF], F32, at=B_LAST_AT) for half in range(2)]
        a_biased = sb("a_biased", [P, SLOTS, S], F32)
        gated = sb("gated", [P, SLOTS, S], F32)

        def v_plane(s, cols):
            return planes[s][:, :V_PLANE].bitcast(U8)[:, cols]

        def make_b(t, cols):
            bank = psum.tile([P, HALF], F32, name="bank")
            for s in range(PASSES):
                nc.tensor.matmul_mx(
                    out=bank[:],
                    lhsT=wb_codes[:, s, 64 * t : 64 * (t + 1)].bitcast(U8).bitcast(FP4X4),
                    lhsT_scale=planes[s][:, V_PLANE + 32 * t : V_PLANE + 32 * (t + 1)].bitcast(U8),
                    rhs=v_words[s][:, cols].bitcast(FP8X4),
                    rhs_scale=v_plane(s, cols),
                    start=(s == 0),
                    stop=(s == PASSES - 1),
                )
            return bank

        def make_a(t, cols):
            bank = psum.tile([P, HALF], F32, name="bank")
            for s in range(PASSES):
                nc.tensor.matmul_mx(
                    out=bank[:],
                    lhsT=wa_codes[s][:, t * P : (t + 1) * P].bitcast(FP8X4),
                    lhsT_scale=wa_scales[s][:, t * P : (t + 1) * P],
                    rhs=v_words[s][:, cols].bitcast(FP8X4),
                    rhs_scale=v_plane(s, cols),
                    start=(s == 0),
                    stop=(s == PASSES - 1),
                )
            nc.scalar.activation(a_biased[:, t, cols], bank[:], IDENT, bias=ba_cols[:, t : t + 1])

        def gate(t, first, count, b_part):
            nc.vector.tensor_tensor(
                gated[:, t, first : first + count], gates[t][:].indirect(picks(first, count)), b_part, MULT
            )

        halves = [slice(0, HALF), slice(HALF, S)]
        last_slot = SLOTS - 1
        for t in range(last_slot):
            for cols in halves:
                nc.scalar.copy(b_sums[:, t, cols], make_b(t, cols)[:])
            gate(t, 0, S, b_sums[:, t, :])
        nc.scalar.copy(b_last[0][:], make_b(last_slot, halves[0])[:])
        b_last_bank = make_b(last_slot, halves[1])
        for cols in halves:
            for t in range(SLOTS):
                make_a(t, cols)

        wo_bf = sb("wo_bf", [P, N, SLOTS], BF16)
        wo_codes = sb("wo_codes", [P, N], U32)
        wo_scales = sb("wo_scales", [P, N], U8)
        out_rows = [slice(c * P, (c + 1) * P) for c in range(OUT_TILES)]
        def quantise_wo(c):
            rows = out_rows[c]
            nc.vector.quantize_mx(
                out=wo_codes[:, rows].bitcast(FP8X4),
                scales=wo_scales[:, rows],
                in_=wo_bf[:, rows, :].rearrange("p n t -> p (n t)"),
            )

        result = sb("result", [P, OUT_TILES, S], F32)
        out_view = out.rearrange("(c p) j -> p c j", p=P)
        starts = [sum(OUT_CHUNKS[:i]) for i in range(len(OUT_CHUNKS))]
        last = len(OUT_CHUNKS) - 1
        h_bf, h_codes, h_scales = {}, {}, {}

        def make_h(i):
            width = OUT_CHUNKS[i]
            h_bf[i] = sb(f"h_bf{i}", [P, width, SLOTS], BF16)
            h_codes[i] = sb(f"h_codes{i}", [P, width], U32)
            h_scales[i] = sb(f"h_scales{i}", [P, width], U8)
            count = min(width, PIECE)
            for first in range(0, width, count):
                part = slice(starts[i] + first, starts[i] + first + count)
                nc.vector.tensor_tensor(
                    h_bf[i][:, first : first + count, :].rearrange("p (n i) t -> p n t i", i=4),
                    a_biased[:, :, part].rearrange("p t (n i) -> p n t i", i=4),
                    gated[:, :, part].rearrange("p t (n i) -> p n t i", i=4),
                    MULT,
                )

        def quantise_h(i):
            nc.vector.quantize_mx(
                out=h_codes[i][:].bitcast(FP8X4),
                scales=h_scales[i][:],
                in_=h_bf[i][:].rearrange("p n t -> p (n t)"),
            )

        def finish(i):
            count = OUT_CHUNKS[i]
            cols = slice(starts[i], starts[i] + count)
            by_tile = i in (0, last)
            stored = slice(starts[last - 1], S) if i == last else cols
            for c, rows in enumerate(out_rows):
                bank = psum.tile([P, count], F32, name="bank")
                nc.tensor.matmul_mx(
                    out=bank[:],
                    lhsT=wo_codes[:, rows].bitcast(FP8X4),
                    lhsT_scale=wo_scales[:, rows],
                    rhs=h_codes[i][:].bitcast(FP8X4),
                    rhs_scale=h_scales[i][:],
                    start=True,
                    stop=True,
                )
                if (i, c) in ((last - 1, 2), (last, 1)):
                    nc.vector.tensor_scalar_add(result[:, c, cols], bank[:], bo_cols[:, c : c + 1])
                else:
                    nc.scalar.activation(
                        result[:, c, cols], bank[:], IDENT, bias=bo_cols[:, c : c + 1]
                    )
                if by_tile:
                    queue = nc.scalar if (i, c) == (last, OUT_TILES - 1) else nc.sync
                    queue.dma_start(out_view[:, c, stored], result[:, c, stored])
            if not by_tile and i != last - 1:
                nc.sync.dma_start(out_view[:, :, cols], result[:, :, cols])

        for first in range(0, HALF, PIECE):
            gate(last_slot, first, PIECE, b_last[0][:, first : first + PIECE])
        nc.scalar.copy(b_last[1][:], b_last_bank[:])
        for rows in out_rows:
            nc.scalar.copy(
                wo_bf[:, rows, :].rearrange("p (n i) t -> p n t i", i=4),
                wo_raw[:, :, rows].rearrange("p t (n i) -> p n t i", i=4),
            )
        make_h(0)
        quantise_h(0)
        quantise_wo(0)
        for piece in range(2):
            first = piece * PIECE
            gate(last_slot, HALF + first, PIECE, b_last[1][:, first : first + PIECE])
            quantise_wo(piece + 1)
        finish(0)
        make_h(1)
        for i in range(2, last + 1):
            make_h(i)
            quantise_h(i - 1)
            finish(i - 1)
        quantise_h(last)
        finish(last)
